import numpy as np
import ml_dtypes


def mxq(x, axis, fmt="e4m3"):
    dtype, down = {"e4m3": (ml_dtypes.float8_e4m3fn, 7), "e5m2": (ml_dtypes.float8_e5m2, 14)}[fmt]
    v = np.moveaxis(np.asarray(x, np.float32).astype(ml_dtypes.bfloat16).astype(np.float64), axis, -1)
    blocks = v.reshape(v.shape[:-1] + (-1, 32))
    amax = np.abs(blocks).max(-1, keepdims=True)
    byte = np.maximum(np.where(amax > 0, np.frexp(amax)[1] - 1 + 127, 0) - down, 1)
    scale = np.exp2(byte - 127.0)
    codes = (blocks / scale).astype(np.float32).astype(dtype).astype(np.float64)
    return np.moveaxis((codes * scale).reshape(v.shape), -1, axis)


WIDE = False


def mx_kscale(k):
    if not WIDE:
        return np.ones(k)
    levels = np.array([10, -10, 5, -5, 0])
    if k % 512:
        return np.exp2(np.random.permutation(np.resize(levels, k // 32))).repeat(32)
    a = np.empty((k // 512, 16))
    for p in range(k // 512):
        a[p, :8] = np.random.permutation(np.resize(levels, 8))
        for g in range(8):
            far = levels[np.abs(levels - a[p, g]) >= 10]
            a[p, g + 8] = far[np.random.randint(len(far))]
    return np.exp2(a.ravel()).repeat(32)


def f64(x):
    return np.asarray(x).astype(np.float64)


def striped(idx):
    return np.tile(idx.reshape(-1, 16).T, (8, 1)).astype(np.uint16)


def unstriped(offs):
    return offs[:16].T.reshape(-1).astype(np.int64)


E2M1 = np.array([0.0, 0.5, 1.0, 1.5, 2.0, 3.0, 4.0, 6.0, -0.0, -0.5, -1.0, -1.5, -2.0, -3.0, -4.0, -6.0])


def pack_fp4(w):
    k, n = w.shape
    w = f64(np.asarray(w, np.float32).astype(ml_dtypes.bfloat16)).reshape(k // 32, 32, n)
    amax = np.abs(w).max(1)
    mant, ex = np.frexp(amax / 6.0)
    byte = np.clip(np.where(amax > 0, np.where(mant > 0.5, ex, ex - 1) + 127, 1), 1, 254)
    scaled = (w * np.exp2(127.0 - byte)[:, None, :]).reshape(k, n).astype(np.float32)
    c = np.ascontiguousarray(scaled.reshape(k // 512, 128, 4, n).transpose(0, 1, 3, 2)).astype(ml_dtypes.float4_e2m1fn).view(np.uint8) & 0xF
    words = (c[..., 0::2] | (c[..., 1::2] << 4)).reshape(k // 512, 128, 2 * n)
    return np.ascontiguousarray(words), np.ascontiguousarray(byte.astype(np.uint8).reshape(k // 512, 16, n))


def unpack_fp4(words, scales):
    g, _, n = scales.shape
    words = np.ascontiguousarray(words).reshape(g, 128, n, 2)
    nib = np.empty((g, 128, n, 4), np.uint8)
    nib[..., 0::2] = words & 0xF
    nib[..., 1::2] = words >> 4
    vals = E2M1[nib] * np.repeat(np.exp2(scales.astype(np.float64) - 127.0), 8, axis=1)[..., None]
    return vals.transpose(0, 1, 3, 2).reshape(g * 512, n)


K, T, S, D, V, N = 1024, 2048, 1024, 3, 512, 256
P = 2 ** 7


def setup_inputs():
    n = np.random.standard_normal
    s = mx_kscale(K)[:, None]
    packed_w1 = pack_fp4(n((K, N)) / np.sqrt(K) / s)
    return {
        "xT": (n((K, T)) * s).astype(np.float32),
        "w1_words": packed_w1[0],
        "w1_scales": packed_w1[1],
        "score": np.tile(np.random.standard_normal((D, 1, V)), (1, P, 1)).astype(np.float32),
        "offs": striped(np.random.permutation(T)[:S]),
        "pos1": striped(np.random.permutation(S)[:V]),
        "pos2": striped(np.random.permutation(S)[:V]),
        "pos3": striped(np.random.permutation(S)[:V]),
    }


def reference(xT, w1_words, w1_scales, score, offs, pos1, pos2, pos3):
    xq = mxq(f64(xT)[:, unstriped(offs)], 0, "e4m3")
    y = unpack_fp4(w1_words, w1_scales).T @ xq
    e0 = np.exp(f64(score)[0, :1])
    e1 = np.exp(f64(score)[1, :1])
    e2 = np.exp(f64(score)[2, :1])
    num = y[:, unstriped(pos1)] * e0 + y[:, unstriped(pos2)] * e1 + y[:, unstriped(pos3)] * e2
    den = e0 + e1 + e2
    return num / den

@@ -1,0 +1,209 @@
+from contextlib import ExitStack
+
+import concourse.mybir as mybir
+from concourse.masks import make_identity
+
+K, T, S, D, V, N = 1024, 2048, 1024, 3, 512, 256
+FLOPS = 2 * K * N * S
+BYTES = K * T * 4 + N * V * 4 + K * N // 2 + K * N // 32 + D * V * 4
+
+F32 = mybir.dt.float32
+BF16 = mybir.dt.bfloat16
+I32 = mybir.dt.int32
+U32 = mybir.dt.uint32
+U16 = mybir.dt.uint16
+U8 = mybir.dt.uint8
+FP8X4 = mybir.dt.float8_e4m3fn_x4
+FP4X4 = mybir.dt.float4_e2m1fn_x4
+ALU = mybir.AluOpType
+ACT = mybir.ActivationFunctionType
+AXIS = mybir.AxisListType
+
+P = 128
+PASSES = K // 512
+BLOCKS = N // P
+BANK = 512
+HALF = V // 2
+SLICE = 256
+STAGE_TAGS = ["bank5", "bank6", "bank7", "bank2", "bank3"]
+
+CHUNKS = [
+    [(1024, 640), (1024, 704)],
+    [(1024, 0), (1024, 704)],
+    [(512, 0), (512, 0), (512, 0), (512, 0)],
+    [(512, 0), (512, 0), (512, 0), (512, 352)],
+]
+
+
+def tile_picked_gatv_none_e_kernel(tc, xT, w1_words, w1_scales, score, offs, pos1, pos2, pos3, out):
+    nc = tc.nc
+    with ExitStack() as ctx:
+        lists = ctx.enter_context(tc.tile_pool(name="lists", bufs=1))
+        keep = ctx.enter_context(tc.tile_pool(name="keep", bufs=1))
+        psum = ctx.enter_context(tc.psum_pool(name="psum", bufs=1))
+
+        def bank(tag):
+            return psum.tile([P, BANK], F32, name=tag, tag=tag)
+
+        x_rows = xT.rearrange("(z p u e) t -> z u p e t", p=P, u=2, e=2)
+        offs_t = lists.tile([P, S // 16], U16, name="offs_t")
+        pos_t = [lists.tile([P, V // 16], U16, name="pos_t%d" % d) for d in range(D)]
+        score_rows = keep.tile([P, D, P], F32, name="score_rows")
+        w_words = keep.tile([P, PASSES, 2 * N], U8, name="w_words", align_bytes=64)
+        w_scales = keep.tile([P, PASSES, N], U8, name="w_scales", align_bytes=64)
+        ident = keep.tile([P, P], F32, name="ident")
+
+        nc.gpsimd.memset(score_rows[:], 0.0)
+        nc.sync.dma_start(score_rows[0 : V // P, :, :], score[:, 0, :].rearrange("d (t c) -> t d c", c=P))
+        nc.sync.dma_start(offs_t[:], offs)
+        make_identity(nc, ident[:])
+        nc.gpsimd.memset(w_scales[:].rearrange("p z n -> p (z n)").bitcast(I32), 0)
+
+        raw = []
+        for pair in range(2 * PASSES):
+            z, u = divmod(pair, 2)
+            c0 = 0
+            row = []
+            for j, (width, share) in enumerate(CHUNKS[pair]):
+                chunk = keep.tile([P, 2, width], F32, name="raw%d_%d" % (pair, j))
+                nc.sync.dma_start(chunk[:], x_rows[z, u, :, :, c0 : c0 + width])
+                row.append((chunk, c0, width, share))
+                c0 = c0 + width
+            raw.append(row)
+        nc.sync.dma_start(w_words[:], w1_words.rearrange("z p n -> p z n"))
+        for q in range(4):
+            nc.sync.dma_start(
+                w_scales[32 * q : 32 * q + 4, :, :].bitcast(I32),
+                w1_scales[:, 4 * q : 4 * q + 4, :].rearrange("z r n -> r z n").bitcast(I32),
+            )
+        for tile, src in zip(pos_t, (pos1, pos2, pos3)):
+            nc.sync.dma_start(tile[:], src)
+
+        vt_count = V // P
+        turned = bank("bank4")
+        for d in range(D):
+            nc.tensor.transpose(turned[:, d * P : (d + 1) * P], score_rows[:, d, :], ident[:])
+        scores = turned[:, 0 : D * P].rearrange("p (d c) -> p c d", c=P)[:, 0:vt_count, :]
+        top = keep.tile([P, vt_count], F32, name="top")
+        shifted = keep.tile([P, vt_count, D], F32, name="shifted")
+        expd = keep.tile([P, vt_count, D], F32, name="expd")
+        total = keep.tile([P, vt_count], F32, name="total")
+        inverse = keep.tile([P, vt_count], F32, name="inverse", tag="early", align_bytes=64)
+        weight = keep.tile([P, vt_count, D], F32, name="weight")
+        nc.vector.tensor_reduce(top[:], scores, AXIS.X, ALU.max)
+        nc.vector.tensor_tensor(shifted[:], scores, top[:].unsqueeze(2).to_broadcast([P, vt_count, D]), ALU.subtract)
+        nc.scalar.activation(expd[:], shifted[:], ACT.Exp)
+        nc.vector.tensor_reduce(total[:], expd[:], AXIS.X, ALU.add)
+        nc.vector.reciprocal(inverse[:], total[:])
+        nc.vector.tensor_tensor(weight[:], expd[:], inverse[:].unsqueeze(2).to_broadcast([P, vt_count, D]), ALU.mult)
+        spread = bank("bank5")
+        for vt in range(vt_count):
+            nc.tensor.transpose(spread[:, vt * P : (vt + 1) * P], weight[:, vt, D - 1 : D].to_broadcast([P, P]), ident[:])
+        last_weight = keep.tile([P, V], F32, name="last_weight")
+        nc.vector.tensor_copy(last_weight[:], spread[:])
+
+        early = keep.tile([P, 2 * T - 8], U32, name="early", tag="early", align_bytes=64)
+        late = keep.tile([P, 2 * T - 8], U32, name="late", align_bytes=64)
+        words = [early[:, T - 8 : 2 * T - 8], early[:, 0:T], late[:, T - 8 : 2 * T - 8], late[:, 0:T]]
+
+        def round_pair(pair):
+            window = words[pair].bitcast(BF16).rearrange("p (t e) -> p t e", e=2)
+            for chunk, c0, width, share in raw[pair]:
+                cut = width - share
+                if cut > 0:
+                    nc.scalar.copy(window[:, c0 : c0 + cut, :], chunk[:, :, 0:cut].rearrange("p e c -> p c e"))
+                if share > 0:
+                    nc.vector.tensor_copy(window[:, c0 + cut : c0 + width, :], chunk[:, :, cut:width].rearrange("p e c -> p c e"))
+            return words[pair]
+
+        codes = [keep.tile([P, S], U32, name="codes%d" % z, align_bytes=64) for z in range(PASSES)]
+        scales = [keep.tile([P, S], U8, name="scales%d" % z, align_bytes=64) for z in range(PASSES)]
+
+        def quantise(z, woven, j0, width):
+            nc.vector.quantize_mx(
+                out=codes[z][:, j0 : j0 + width].bitcast(FP8X4),
+                scales=scales[z][:, j0 : j0 + width],
+                in_=woven,
+            )
+
+        picked0 = [keep.tile([P, 2, BANK], U32, name="picked0_%d" % h) for h in range(2)]
+        for u in range(2):
+            window = round_pair(u)
+            for h in range(2):
+                nc.vector.tensor_copy(picked0[h][:, u, :], window.indirect(offs_t[:, h * BANK // 16 : (h + 1) * BANK // 16]))
+        woven0 = [keep.tile([P, 2 * BANK], U32, name="woven0_%d" % h, align_bytes=64)[:] for h in range(2)]
+        for h in range(2):
+            nc.vector.tensor_copy(
+                woven0[h].bitcast(I32).rearrange("p (n u) -> p n u", u=2),
+                picked0[h][:].bitcast(I32).rearrange("p u n -> p n u"),
+            )
+        for h in range(2):
+            quantise(0, woven0[h].bitcast(BF16), h * BANK, BANK)
+
+        slices = S // SLICE
+        picked1 = [keep.tile([P, 2, SLICE], U32, name="picked1_%d" % s) for s in range(slices)]
+        woven1 = [keep.tile([P, 4 * SLICE], BF16, name="woven1_%d" % s, align_bytes=64) for s in range(slices)]
+        for u in range(2):
+            window = round_pair(2 + u)
+            for s in range(slices):
+                nc.vector.tensor_copy(picked1[s][:, u, :], window.indirect(offs_t[:, s * SLICE // 16 : (s + 1) * SLICE // 16]))
+        for s in range(slices):
+            nc.scalar.copy(woven1[s][:].bitcast(U32).rearrange("p (n u) -> p n u", u=2), picked1[s][:].rearrange("p u n -> p n u"))
+        for s in range(slices):
+            quantise(1, woven1[s][:], s * SLICE, SLICE)
+
+        acc = [[bank("bank%d" % (2 * b + h)) for h in range(2)] for b in range(BLOCKS)]
+        for z in range(PASSES):
+            for h in range(2):
+                for b in range(BLOCKS):
+                    nc.tensor.matmul_mx(
+                        out=acc[b][h][:],
+                        lhsT=w_words[:, z, 2 * P * b : 2 * P * (b + 1)].bitcast(FP4X4),
+                        lhsT_scale=w_scales[:, z, P * b : P * (b + 1)],
+                        rhs=codes[z][:, h * BANK : (h + 1) * BANK].bitcast(FP8X4),
+                        rhs_scale=scales[z][:, h * BANK : (h + 1) * BANK],
+                        start=(z == 0),
+                        stop=(z == PASSES - 1),
+                    )
+        y = [keep.tile([P, S], F32, name="y%d" % b) for b in range(BLOCKS)]
+        nc.scalar.copy(y[0][:, 0:BANK], acc[0][0][:])
+        nc.vector.tensor_copy(y[0][:, BANK:S], acc[0][1][:])
+        nc.scalar.copy(y[1][:, 0:BANK], acc[1][0][:])
+        nc.scalar.copy(y[1][:, BANK:S], acc[1][1][:])
+
+        def pos_slice(d, h):
+            return pos_t[d][:, h * HALF // 16 : (h + 1) * HALF // 16]
+
+        def weighted_sum(b, h, count, unit0, target):
+            for d in range(count):
+                name = "%d_%d_%d" % (b, h, d)
+                fetched = keep.tile([P, HALF], F32, name="fetched" + name)
+                nc.vector.tensor_copy(fetched[:], y[b][:].indirect(pos_slice(d, h)))
+                stage = bank(STAGE_TAGS[(unit0 + d) % len(STAGE_TAGS)])
+                for i in range(2):
+                    nc.tensor.transpose(stage[:, i * P : (i + 1) * P], fetched[:, i * P : (i + 1) * P], ident[:])
+                for i in range(2):
+                    piece = keep.tile([P, P], F32, name="scaled%s_%d" % (name, i))
+                    nc.scalar.activation(piece[:], stage[:, i * P : (i + 1) * P], ACT.Copy, scale=weight[:, 2 * h + i, d : d + 1])
+                    nc.tensor.matmul(
+                        target[:, i * P : (i + 1) * P], piece[:], ident[:],
+                        start=(d == 0 and i == 0), stop=(d == count - 1 and i == 1), is_transpose=True,
+                    )
+
+        sums0 = bank("bank4")
+        for h in range(2):
+            weighted_sum(0, h, D, D * h, sums0[:, h * HALF : (h + 1) * HALF])
+        result0 = keep.tile([P, V], F32, name="result0")
+        nc.scalar.copy(result0[:], sums0[:])
+        nc.sync.dma_start(out[0:P, :], result0[:])
+
+        sums1 = [bank("bank%d" % h) for h in range(2)]
+        for h in range(2):
+            weighted_sum(1, h, D - 1, 2 * D + (D - 1) * h, sums1[h][:, 0:HALF])
+        products = [keep.tile([P, HALF], F32, name="product%d" % h) for h in range(2)]
+        for h in range(2):
+            nc.vector.tensor_tensor(products[h][:], y[1][:].indirect(pos_slice(D - 1, h)), last_weight[:, h * HALF : (h + 1) * HALF], ALU.mult)
+        for h in range(2):
+            result1 = keep.tile([P, HALF], F32, name="result1_%d" % h)
+            nc.vector.tensor_tensor(result1[:], sums1[h][:, 0:HALF], products[h][:], ALU.add)
+            nc.sync.dma_start(out[P : 2 * P, h * HALF : (h + 1) * HALF], result1[:])

@@ -23,16 +23,11 @@ P = 128
 PASSES = K // 512
 BLOCKS = N // P
 BANK = 512
-HALF = V // 2
-SLICE = 256
-STAGE_TAGS = ["bank5", "bank6", "bank7", "bank2", "bank3"]
-
-CHUNKS = [
-    [(1024, 640), (1024, 704)],
-    [(1024, 0), (1024, 704)],
-    [(512, 0), (512, 0), (512, 0), (512, 0)],
-    [(512, 0), (512, 0), (512, 0), (512, 352)],
-]
+SLICES = [(0, 512), (512, 256), (768, 128), (896, 128)]
+PIECES = [(0, 0, 256), (0, 256, 256), (1, 0, 256), (2, 0, 128), (3, 0, 128)]
+GROUPS = [[(0, 4)], [(0, 2), (2, 2)]]
+VECTOR_PIECES = [2, 2, 2, 1, 1, 1, 1, 1]
+PER = V // P
 
 
 def tile_picked_gatv_none_e_kernel(tc, xT, w1_words, w1_scales, score, offs, pos1, pos2, pos3, out):
@@ -42,168 +37,132 @@ def tile_picked_gatv_none_e_kernel(tc, xT, w1_words, w1_scales, score, offs, pos
         keep = ctx.enter_context(tc.tile_pool(name="keep", bufs=1))
         psum = ctx.enter_context(tc.psum_pool(name="psum", bufs=1))
 
-        def bank(tag):
-            return psum.tile([P, BANK], F32, name=tag, tag=tag)
+        def bank(i):
+            return psum.tile([P, BANK], F32, name="bank%d" % i, tag="bank%d" % i)
 
-        x_rows = xT.rearrange("(z p u e) t -> z u p e t", p=P, u=2, e=2)
+        x_rows = xT.rearrange("(z p t) c -> z t p c", p=P, t=4)
         offs_t = lists.tile([P, S // 16], U16, name="offs_t")
         pos_t = [lists.tile([P, V // 16], U16, name="pos_t%d" % d) for d in range(D)]
-        score_rows = keep.tile([P, D, P], F32, name="score_rows")
+        scores = keep.tile([P, D, 8], F32, name="scores")
         w_words = keep.tile([P, PASSES, 2 * N], U8, name="w_words", align_bytes=64)
         w_scales = keep.tile([P, PASSES, N], U8, name="w_scales", align_bytes=64)
         ident = keep.tile([P, P], F32, name="ident")
+        planes = [keep.tile([P, T], F32, name="plane%d" % j) for j in range(4 * PASSES)]
 
-        nc.gpsimd.memset(score_rows[:], 0.0)
-        nc.sync.dma_start(score_rows[0 : V // P, :, :], score[:, 0, :].rearrange("d (t c) -> t d c", c=P))
-        nc.sync.dma_start(offs_t[:], offs)
-        make_identity(nc, ident[:])
         nc.gpsimd.memset(w_scales[:].rearrange("p z n -> p (z n)").bitcast(I32), 0)
-
-        raw = []
-        for pair in range(2 * PASSES):
-            z, u = divmod(pair, 2)
-            c0 = 0
-            row = []
-            for j, (width, share) in enumerate(CHUNKS[pair]):
-                chunk = keep.tile([P, 2, width], F32, name="raw%d_%d" % (pair, j))
-                nc.sync.dma_start(chunk[:], x_rows[z, u, :, :, c0 : c0 + width])
-                row.append((chunk, c0, width, share))
-                c0 = c0 + width
-            raw.append(row)
-        nc.sync.dma_start(w_words[:], w1_words.rearrange("z p n -> p z n"))
+        make_identity(nc, ident[:])
+        nc.sync.dma_start(scores[:, :, 0:PER], score[:, 0, :].rearrange("d (p j) -> p d j", j=PER))
+        nc.sync.dma_start(planes[0][:], x_rows[0, 0])
+        nc.sync.dma_start(offs_t[:], offs)
         for q in range(4):
-            nc.sync.dma_start(
+            nc.scalar.dma_start(
                 w_scales[32 * q : 32 * q + 4, :, :].bitcast(I32),
                 w1_scales[:, 4 * q : 4 * q + 4, :].rearrange("z r n -> r z n").bitcast(I32),
             )
+        for j in range(1, 4 * PASSES):
+            nc.sync.dma_start(planes[j][:], x_rows[j // 4, j % 4])
+            if j == 6:
+                nc.sync.dma_start(w_words[:], w1_words.rearrange("z p n -> p z n"))
         for tile, src in zip(pos_t, (pos1, pos2, pos3)):
             nc.sync.dma_start(tile[:], src)
 
-        vt_count = V // P
-        turned = bank("bank4")
-        for d in range(D):
-            nc.tensor.transpose(turned[:, d * P : (d + 1) * P], score_rows[:, d, :], ident[:])
-        scores = turned[:, 0 : D * P].rearrange("p (d c) -> p c d", c=P)[:, 0:vt_count, :]
-        top = keep.tile([P, vt_count], F32, name="top")
-        shifted = keep.tile([P, vt_count, D], F32, name="shifted")
-        expd = keep.tile([P, vt_count, D], F32, name="expd")
-        total = keep.tile([P, vt_count], F32, name="total")
-        inverse = keep.tile([P, vt_count], F32, name="inverse", tag="early", align_bytes=64)
-        weight = keep.tile([P, vt_count, D], F32, name="weight")
-        nc.vector.tensor_reduce(top[:], scores, AXIS.X, ALU.max)
-        nc.vector.tensor_tensor(shifted[:], scores, top[:].unsqueeze(2).to_broadcast([P, vt_count, D]), ALU.subtract)
+        by_target = scores[:, :, 0:PER].rearrange("p d j -> p j d")
+        top = keep.tile([P, PER], F32, name="top")
+        shifted = keep.tile([P, PER, D], F32, name="shifted")
+        expd = keep.tile([P, PER, D], F32, name="expd")
+        total = keep.tile([P, PER], F32, name="total")
+        inverse = keep.tile([P, PER], F32, name="inverse")
+        weight = keep.tile([P, PER, D], F32, name="weight")
+        nc.vector.tensor_reduce(top[:], by_target, AXIS.X, ALU.max)
+        nc.vector.tensor_tensor(shifted[:], by_target, top[:].unsqueeze(2).to_broadcast([P, PER, D]), ALU.subtract)
         nc.scalar.activation(expd[:], shifted[:], ACT.Exp)
         nc.vector.tensor_reduce(total[:], expd[:], AXIS.X, ALU.add)
         nc.vector.reciprocal(inverse[:], total[:])
-        nc.vector.tensor_tensor(weight[:], expd[:], inverse[:].unsqueeze(2).to_broadcast([P, vt_count, D]), ALU.mult)
-        spread = bank("bank5")
-        for vt in range(vt_count):
-            nc.tensor.transpose(spread[:, vt * P : (vt + 1) * P], weight[:, vt, D - 1 : D].to_broadcast([P, P]), ident[:])
-        last_weight = keep.tile([P, V], F32, name="last_weight")
-        nc.vector.tensor_copy(last_weight[:], spread[:])
+        nc.vector.tensor_tensor(weight[:], expd[:], inverse[:].unsqueeze(2).to_broadcast([P, PER, D]), ALU.mult)
+        weight_rows = []
+        for d in range(D):
+            spread = bank(d)
+            for j in range(PER):
+                nc.tensor.transpose(spread[:, j * P : (j + 1) * P], weight[:, j, d : d + 1].to_broadcast([P, P]), ident[:])
+            row = keep.tile([P, V], F32, name="weight_row%d" % d)
+            nc.vector.tensor_copy(row[:].rearrange("q (p j) -> q p j", j=PER), spread[:].rearrange("q (j p) -> q p j", j=PER))
+            weight_rows.append(row)
 
-        early = keep.tile([P, 2 * T - 8], U32, name="early", tag="early", align_bytes=64)
-        late = keep.tile([P, 2 * T - 8], U32, name="late", align_bytes=64)
-        words = [early[:, T - 8 : 2 * T - 8], early[:, 0:T], late[:, T - 8 : 2 * T - 8], late[:, 0:T]]
-
-        def round_pair(pair):
-            window = words[pair].bitcast(BF16).rearrange("p (t e) -> p t e", e=2)
-            for chunk, c0, width, share in raw[pair]:
-                cut = width - share
-                if cut > 0:
-                    nc.scalar.copy(window[:, c0 : c0 + cut, :], chunk[:, :, 0:cut].rearrange("p e c -> p c e"))
-                if share > 0:
-                    nc.vector.tensor_copy(window[:, c0 + cut : c0 + width, :], chunk[:, :, cut:width].rearrange("p e c -> p c e"))
-            return words[pair]
-
-        codes = [keep.tile([P, S], U32, name="codes%d" % z, align_bytes=64) for z in range(PASSES)]
-        scales = [keep.tile([P, S], U8, name="scales%d" % z, align_bytes=64) for z in range(PASSES)]
-
-        def quantise(z, woven, j0, width):
-            nc.vector.quantize_mx(
-                out=codes[z][:, j0 : j0 + width].bitcast(FP8X4),
-                scales=scales[z][:, j0 : j0 + width],
-                in_=woven,
-            )
-
-        picked0 = [keep.tile([P, 2, BANK], U32, name="picked0_%d" % h) for h in range(2)]
-        for u in range(2):
-            window = round_pair(u)
-            for h in range(2):
-                nc.vector.tensor_copy(picked0[h][:, u, :], window.indirect(offs_t[:, h * BANK // 16 : (h + 1) * BANK // 16]))
-        woven0 = [keep.tile([P, 2 * BANK], U32, name="woven0_%d" % h, align_bytes=64)[:] for h in range(2)]
-        for h in range(2):
-            nc.vector.tensor_copy(
-                woven0[h].bitcast(I32).rearrange("p (n u) -> p n u", u=2),
-                picked0[h][:].bitcast(I32).rearrange("p u n -> p n u"),
-            )
-        for h in range(2):
-            quantise(0, woven0[h].bitcast(BF16), h * BANK, BANK)
-
-        slices = S // SLICE
-        picked1 = [keep.tile([P, 2, SLICE], U32, name="picked1_%d" % s) for s in range(slices)]
-        woven1 = [keep.tile([P, 4 * SLICE], BF16, name="woven1_%d" % s, align_bytes=64) for s in range(slices)]
-        for u in range(2):
-            window = round_pair(2 + u)
-            for s in range(slices):
-                nc.vector.tensor_copy(picked1[s][:, u, :], window.indirect(offs_t[:, s * SLICE // 16 : (s + 1) * SLICE // 16]))
-        for s in range(slices):
-            nc.scalar.copy(woven1[s][:].bitcast(U32).rearrange("p (n u) -> p n u", u=2), picked1[s][:].rearrange("p u n -> p n u"))
-        for s in range(slices):
-            quantise(1, woven1[s][:], s * SLICE, SLICE)
-
-        acc = [[bank("bank%d" % (2 * b + h)) for h in range(2)] for b in range(BLOCKS)]
+        count = len(SLICES)
+        acc = [[None] * count for b in range(BLOCKS)]
         for z in range(PASSES):
-            for h in range(2):
+            woven = [keep.tile([P, n, 4], BF16, name="woven%d_%d" % (z, s), align_bytes=64) for s, (j0, n) in enumerate(SLICES)]
+            codes = [keep.tile([P, n], U32, name="codes%d_%d" % (z, s), align_bytes=64) for s, (j0, n) in enumerate(SLICES)]
+            scales = [keep.tile([P, n], U8, name="scales%d_%d" % (z, s), align_bytes=64) for s, (j0, n) in enumerate(SLICES)]
+
+            def finish(s):
+                nc.vector.quantize_mx(
+                    out=codes[s][:].bitcast(FP8X4), scales=scales[s][:], in_=woven[s][:].rearrange("p n t -> p (n t)")
+                )
                 for b in range(BLOCKS):
+                    if z == 0:
+                        acc[b][s] = bank(count * b + s)
                     nc.tensor.matmul_mx(
-                        out=acc[b][h][:],
+                        out=acc[b][s][:, 0 : SLICES[s][1]],
                         lhsT=w_words[:, z, 2 * P * b : 2 * P * (b + 1)].bitcast(FP4X4),
                         lhsT_scale=w_scales[:, z, P * b : P * (b + 1)],
-                        rhs=codes[z][:, h * BANK : (h + 1) * BANK].bitcast(FP8X4),
-                        rhs_scale=scales[z][:, h * BANK : (h + 1) * BANK],
+                        rhs=codes[s][:].bitcast(FP8X4),
+                        rhs_scale=scales[s][:],
                         start=(z == 0),
                         stop=(z == PASSES - 1),
                     )
-        y = [keep.tile([P, S], F32, name="y%d" % b) for b in range(BLOCKS)]
-        nc.scalar.copy(y[0][:, 0:BANK], acc[0][0][:])
-        nc.vector.tensor_copy(y[0][:, BANK:S], acc[0][1][:])
-        nc.scalar.copy(y[1][:, 0:BANK], acc[1][0][:])
-        nc.scalar.copy(y[1][:, BANK:S], acc[1][1][:])
 
-        def pos_slice(d, h):
-            return pos_t[d][:, h * HALF // 16 : (h + 1) * HALF // 16]
+            for t0, width in GROUPS[z]:
+                tags = ["picked%d_%d_%d" % (z, t0, i) for i in range(len(PIECES))]
+                if z == 1 and t0 == 0:
+                    tags[0] = "woven0_%d" % (count - 1)
+                if z == 1 and t0 == 2:
+                    tags[0] = "picked1_0_4"
+                picked = [keep.tile([P, width, n], BF16, name="picked%d_%d_%d" % (z, t0, i), tag=tags[i], align_bytes=64) for i, (s, c0, n) in enumerate(PIECES)]
+                for e in range(width):
+                    j = 4 * z + t0 + e
+                    for i, (s, c0, n) in enumerate(PIECES):
+                        j0 = SLICES[s][0] + c0
+                        looked_up = planes[j][:].indirect(offs_t[:, j0 // 16 : (j0 + n) // 16])
+                        if i < VECTOR_PIECES[j]:
+                            nc.vector.tensor_copy(picked[i][:, e, :], looked_up)
+                        else:
+                            nc.scalar.activation(picked[i][:, e, :], looked_up, ACT.Copy)
+                for i, (s, c0, n) in enumerate(PIECES):
+                    nc.vector.tensor_copy(woven[s][:, c0 : c0 + n, t0 : t0 + width], picked[i][:].rearrange("p e n -> p n e"))
+                    if t0 + width == 4 and s > 0:
+                        finish(s - 1)
+            finish(count - 1)
 
-        def weighted_sum(b, h, count, unit0, target):
-            for d in range(count):
-                name = "%d_%d_%d" % (b, h, d)
-                fetched = keep.tile([P, HALF], F32, name="fetched" + name)
-                nc.vector.tensor_copy(fetched[:], y[b][:].indirect(pos_slice(d, h)))
-                stage = bank(STAGE_TAGS[(unit0 + d) % len(STAGE_TAGS)])
-                for i in range(2):
-                    nc.tensor.transpose(stage[:, i * P : (i + 1) * P], fetched[:, i * P : (i + 1) * P], ident[:])
-                for i in range(2):
-                    piece = keep.tile([P, P], F32, name="scaled%s_%d" % (name, i))
-                    nc.scalar.activation(piece[:], stage[:, i * P : (i + 1) * P], ACT.Copy, scale=weight[:, 2 * h + i, d : d + 1])
-                    nc.tensor.matmul(
-                        target[:, i * P : (i + 1) * P], piece[:], ident[:],
-                        start=(d == 0 and i == 0), stop=(d == count - 1 and i == 1), is_transpose=True,
-                    )
+        y = [
+            keep.tile([P, S], F32, name="y0", align_bytes=64),
+            keep.tile([P, S], F32, name="y1", align_bytes=64),
+        ]
+        for s, (j0, n) in enumerate(SLICES):
+            nc.scalar.copy(y[0][:, j0 : j0 + n], acc[0][s][:, 0:n])
+            if s == 0:
+                nc.scalar.copy(y[1][:, j0 : j0 + n], acc[1][s][:, 0:n])
+        for s, (j0, n) in enumerate(SLICES):
+            if s > 0:
+                nc.vector.tensor_copy(y[1][:, j0 : j0 + n], acc[1][s][:, 0:n])
 
-        sums0 = bank("bank4")
-        for h in range(2):
-            weighted_sum(0, h, D, D * h, sums0[:, h * HALF : (h + 1) * HALF])
-        result0 = keep.tile([P, V], F32, name="result0")
-        nc.scalar.copy(result0[:], sums0[:])
-        nc.sync.dma_start(out[0:P, :], result0[:])
-
-        sums1 = [bank("bank%d" % h) for h in range(2)]
-        for h in range(2):
-            weighted_sum(1, h, D - 1, 2 * D + (D - 1) * h, sums1[h][:, 0:HALF])
-        products = [keep.tile([P, HALF], F32, name="product%d" % h) for h in range(2)]
-        for h in range(2):
-            nc.vector.tensor_tensor(products[h][:], y[1][:].indirect(pos_slice(D - 1, h)), last_weight[:, h * HALF : (h + 1) * HALF], ALU.mult)
-        for h in range(2):
-            result1 = keep.tile([P, HALF], F32, name="result1_%d" % h)
-            nc.vector.tensor_tensor(result1[:], sums1[h][:, 0:HALF], products[h][:], ALU.add)
-            nc.sync.dma_start(out[P : 2 * P, h * HALF : (h + 1) * HALF], result1[:])
+        for b, v0, n, fused in ((0, 0, 512, 1), (1, 0, 256, 0), (1, 256, 256, 0)):
+            cols = slice(v0, v0 + n)
+            terms = []
+            for d in range(D):
+                name = "%d_%d_%d" % (b, v0, d)
+                looked_up = y[b][:].indirect(pos_t[d][:, v0 // 16 : (v0 + n) // 16])
+                term = keep.tile([P, n], F32, name="term" + name)
+                if d < fused:
+                    nc.vector.tensor_tensor(term[:], looked_up, weight_rows[d][:, cols], ALU.mult)
+                else:
+                    fetched = keep.tile([P, n], F32, name="fetched" + name)
+                    nc.scalar.activation(fetched[:], looked_up, ACT.Copy)
+                    nc.vector.tensor_tensor(term[:], fetched[:], weight_rows[d][:, cols], ALU.mult)
+                terms.append(term)
+                if d == 1:
+                    partial = keep.tile([P, n], F32, name="partial%d_%d" % (b, v0))
+                    nc.vector.tensor_tensor(partial[:], terms[0][:], terms[1][:], ALU.add)
+            result = keep.tile([P, n], F32, name="result%d_%d" % (b, v0))
+            nc.vector.tensor_tensor(result[:], partial[:], terms[2][:], ALU.add)
+            nc.sync.dma_start(out[b * P : (b + 1) * P, cols], result[:])

@@ -23,11 +23,13 @@ P = 128
 PASSES = K // 512
 BLOCKS = N // P
 BANK = 512
-SLICES = [(0, 512), (512, 256), (768, 128), (896, 128)]
-PIECES = [(0, 0, 256), (0, 256, 256), (1, 0, 256), (2, 0, 128), (3, 0, 128)]
-GROUPS = [[(0, 4)], [(0, 2), (2, 2)]]
-VECTOR_PIECES = [2, 2, 2, 1, 1, 1, 1, 1]
 PER = V // P
+SLICES = [(0, 256), (256, 256), (512, 256), (768, 128), (896, 128)]
+PIECES = [(0, 0, 128), (0, 128, 128), (1, 0, 256), (2, 0, 256), (3, 0, 128), (4, 0, 128)]
+BANKS = [[[0, 1], [2, 3], [4]], [[0, 1], [2, 3, 4]]]
+GROUPS = [[(0, 4)], [(0, 2), (2, 2)]]
+VECTOR_PIECES = [[0, 1, 2], [0, 1, 2], [0, 1, 2], [0, 1], [0, 1], [0, 1], [0, 1], [0]]
+UNITS = ((0, 0, 256, 1, 2), (0, 256, 256, 1, 2), (1, 0, 256, 1, 2), (1, 256, 256, 0, 0))
 
 
 def tile_picked_gatv_none_e_kernel(tc, xT, w1_words, w1_scales, score, offs, pos1, pos2, pos3, out):
@@ -49,20 +51,19 @@ def tile_picked_gatv_none_e_kernel(tc, xT, w1_words, w1_scales, score, offs, pos
         ident = keep.tile([P, P], F32, name="ident")
         planes = [keep.tile([P, T], F32, name="plane%d" % j) for j in range(4 * PASSES)]
 
-        nc.gpsimd.memset(w_scales[:].rearrange("p z n -> p (z n)").bitcast(I32), 0)
         make_identity(nc, ident[:])
+        nc.gpsimd.memset(w_scales[:].rearrange("p z n -> p (z n)").bitcast(I32), 0)
         nc.sync.dma_start(scores[:, :, 0:PER], score[:, 0, :].rearrange("d (p j) -> p d j", j=PER))
-        nc.sync.dma_start(planes[0][:], x_rows[0, 0])
-        nc.sync.dma_start(offs_t[:], offs)
+        for j in range(4 * PASSES):
+            nc.sync.dma_start(planes[j][:], x_rows[j // 4, j % 4])
+            if j == 0:
+                nc.sync.dma_start(offs_t[:], offs)
+        nc.sync.dma_start(w_words[:], w1_words.rearrange("z p n -> p z n"))
         for q in range(4):
-            nc.scalar.dma_start(
+            nc.sync.dma_start(
                 w_scales[32 * q : 32 * q + 4, :, :].bitcast(I32),
                 w1_scales[:, 4 * q : 4 * q + 4, :].rearrange("z r n -> r z n").bitcast(I32),
             )
-        for j in range(1, 4 * PASSES):
-            nc.sync.dma_start(planes[j][:], x_rows[j // 4, j % 4])
-            if j == 6:
-                nc.sync.dma_start(w_words[:], w1_words.rearrange("z p n -> p z n"))
         for tile, src in zip(pos_t, (pos1, pos2, pos3)):
             nc.sync.dma_start(tile[:], src)
 
@@ -84,12 +85,10 @@ def tile_picked_gatv_none_e_kernel(tc, xT, w1_words, w1_scales, score, offs, pos
             spread = bank(d)
             for j in range(PER):
                 nc.tensor.transpose(spread[:, j * P : (j + 1) * P], weight[:, j, d : d + 1].to_broadcast([P, P]), ident[:])
-            row = keep.tile([P, V], F32, name="weight_row%d" % d)
-            nc.vector.tensor_copy(row[:].rearrange("q (p j) -> q p j", j=PER), spread[:].rearrange("q (j p) -> q p j", j=PER))
-            weight_rows.append(row)
+            weight_rows.append(spread[:].rearrange("q (j p) -> q p j", j=PER))
 
         count = len(SLICES)
-        acc = [[None] * count for b in range(BLOCKS)]
+        acc = [[bank(D + len(BANKS[0]) * b + g) for g in range(len(BANKS[b]))] for b in range(BLOCKS)]
         for z in range(PASSES):
             woven = [keep.tile([P, n, 4], BF16, name="woven%d_%d" % (z, s), align_bytes=64) for s, (j0, n) in enumerate(SLICES)]
             codes = [keep.tile([P, n], U32, name="codes%d_%d" % (z, s), align_bytes=64) for s, (j0, n) in enumerate(SLICES)]
@@ -100,16 +99,16 @@ def tile_picked_gatv_none_e_kernel(tc, xT, w1_words, w1_scales, score, offs, pos
                     out=codes[s][:].bitcast(FP8X4), scales=scales[s][:], in_=woven[s][:].rearrange("p n t -> p (n t)")
                 )
                 for b in range(BLOCKS):
-                    if z == 0:
-                        acc[b][s] = bank(count * b + s)
+                    g = [s in group for group in BANKS[b]].index(True)
+                    c0 = SLICES[s][0] - SLICES[BANKS[b][g][0]][0]
                     nc.tensor.matmul_mx(
-                        out=acc[b][s][:, 0 : SLICES[s][1]],
+                        out=acc[b][g][:, c0 : c0 + SLICES[s][1]],
                         lhsT=w_words[:, z, 2 * P * b : 2 * P * (b + 1)].bitcast(FP4X4),
                         lhsT_scale=w_scales[:, z, P * b : P * (b + 1)],
                         rhs=codes[s][:].bitcast(FP8X4),
                         rhs_scale=scales[s][:],
-                        start=(z == 0),
-                        stop=(z == PASSES - 1),
+                        start=(z == 0 and s == BANKS[b][g][0]),
+                        stop=(z == PASSES - 1 and s == BANKS[b][g][-1]),
                     )
 
             for t0, width in GROUPS[z]:
@@ -117,52 +116,63 @@ def tile_picked_gatv_none_e_kernel(tc, xT, w1_words, w1_scales, score, offs, pos
                 if z == 1 and t0 == 0:
                     tags[0] = "woven0_%d" % (count - 1)
                 if z == 1 and t0 == 2:
-                    tags[0] = "picked1_0_4"
+                    tags[0] = "picked1_0_%d" % (len(PIECES) - 1)
                 picked = [keep.tile([P, width, n], BF16, name="picked%d_%d_%d" % (z, t0, i), tag=tags[i], align_bytes=64) for i, (s, c0, n) in enumerate(PIECES)]
                 for e in range(width):
                     j = 4 * z + t0 + e
                     for i, (s, c0, n) in enumerate(PIECES):
                         j0 = SLICES[s][0] + c0
                         looked_up = planes[j][:].indirect(offs_t[:, j0 // 16 : (j0 + n) // 16])
-                        if i < VECTOR_PIECES[j]:
+                        if i in VECTOR_PIECES[j]:
                             nc.vector.tensor_copy(picked[i][:, e, :], looked_up)
                         else:
                             nc.scalar.activation(picked[i][:, e, :], looked_up, ACT.Copy)
+                done = 0
                 for i, (s, c0, n) in enumerate(PIECES):
                     nc.vector.tensor_copy(woven[s][:, c0 : c0 + n, t0 : t0 + width], picked[i][:].rearrange("p e n -> p n e"))
-                    if t0 + width == 4 and s > 0:
-                        finish(s - 1)
+                    if t0 + width == 4 and s > done:
+                        finish(done)
+                        done = done + 1
             finish(count - 1)
 
         y = [
             keep.tile([P, S], F32, name="y0", align_bytes=64),
-            keep.tile([P, S], F32, name="y1", align_bytes=64),
+            keep.tile([P, S], F32, name="y1", tag="woven1_%d" % (count - 1), align_bytes=64),
         ]
-        for s, (j0, n) in enumerate(SLICES):
-            nc.scalar.copy(y[0][:, j0 : j0 + n], acc[0][s][:, 0:n])
-            if s == 0:
-                nc.scalar.copy(y[1][:, j0 : j0 + n], acc[1][s][:, 0:n])
-        for s, (j0, n) in enumerate(SLICES):
-            if s > 0:
-                nc.vector.tensor_copy(y[1][:, j0 : j0 + n], acc[1][s][:, 0:n])
+        for b, g, engine in ((0, 0, "scalar"), (0, 1, "scalar"), (0, 2, "scalar"), (1, 0, "vector"), (1, 1, "vector")):
+            j0 = SLICES[BANKS[b][g][0]][0]
+            n = sum(SLICES[s][1] for s in BANKS[b][g])
+            if engine == "scalar":
+                nc.scalar.copy(y[b][:, j0 : j0 + n], acc[b][g][:, 0:n])
+            else:
+                nc.vector.tensor_copy(y[b][:, j0 : j0 + n], acc[b][g][:, 0:n])
 
-        for b, v0, n, fused in ((0, 0, 512, 1), (1, 0, 256, 0), (1, 256, 256, 0)):
-            cols = slice(v0, v0 + n)
+        held = None
+        for b, v0, n, on_vector, pool_adds in UNITS:
             terms = []
             for d in range(D):
                 name = "%d_%d_%d" % (b, v0, d)
                 looked_up = y[b][:].indirect(pos_t[d][:, v0 // 16 : (v0 + n) // 16])
+                fetched = keep.tile([P, n], F32, name="fetched" + name, tag=held if d < on_vector and held else "fetched" + name)
+                if d == 1:
+                    held = "fetched" + name
                 term = keep.tile([P, n], F32, name="term" + name)
-                if d < fused:
-                    nc.vector.tensor_tensor(term[:], looked_up, weight_rows[d][:, cols], ALU.mult)
+                if d < on_vector:
+                    nc.vector.tensor_copy(fetched[:], looked_up)
                 else:
-                    fetched = keep.tile([P, n], F32, name="fetched" + name)
                     nc.scalar.activation(fetched[:], looked_up, ACT.Copy)
-                    nc.vector.tensor_tensor(term[:], fetched[:], weight_rows[d][:, cols], ALU.mult)
+                nc.vector.tensor_tensor(
+                    term[:].rearrange("q (p j) -> q p j", j=PER),
+                    fetched[:].rearrange("q (p j) -> q p j", j=PER),
+                    weight_rows[d][:, v0 // PER : (v0 + n) // PER, :],
+                    ALU.mult,
+                )
                 terms.append(term)
                 if d == 1:
                     partial = keep.tile([P, n], F32, name="partial%d_%d" % (b, v0))
-                    nc.vector.tensor_tensor(partial[:], terms[0][:], terms[1][:], ALU.add)
+                    adder = nc.gpsimd if pool_adds > 0 else nc.vector
+                    adder.tensor_tensor(partial[:], terms[0][:], terms[1][:], ALU.add)
             result = keep.tile([P, n], F32, name="result%d_%d" % (b, v0))
-            nc.vector.tensor_tensor(result[:], partial[:], terms[2][:], ALU.add)
-            nc.sync.dma_start(out[b * P : (b + 1) * P, cols], result[:])
+            adder = nc.gpsimd if pool_adds > 1 else nc.vector
+            adder.tensor_tensor(result[:], partial[:], terms[2][:], ALU.add)
+            nc.sync.dma_start(out[b * P : (b + 1) * P, v0 : v0 + n], result[:])

@@ -28,8 +28,8 @@ SLICES = [(0, 256), (256, 256), (512, 256), (768, 128), (896, 128)]
 PIECES = [(0, 0, 128), (0, 128, 128), (1, 0, 256), (2, 0, 256), (3, 0, 128), (4, 0, 128)]
 BANKS = [[[0, 1], [2, 3], [4]], [[0, 1], [2, 3, 4]]]
 GROUPS = [[(0, 4)], [(0, 2), (2, 2)]]
-VECTOR_PIECES = [[0, 1, 2], [0, 1, 2], [0, 1, 2], [0, 1], [0, 1], [0, 1], [0, 1], [0]]
-UNITS = ((0, 0, 256, 1, 2), (0, 256, 256, 1, 2), (1, 0, 256, 1, 2), (1, 256, 256, 0, 0))
+VECTOR_PIECES = [[0, 1, 2], [0, 1, 2], [0, 1, 2], [0, 1], [0, 1], [0, 1], [0, 1, 2], [0]]
+UNITS = ((0, 0, 256, 0, 2), (0, 256, 256, 256, 2), (1, 0, 256, 256, 2), (1, 256, 256, 128, 0))
 
 
 def tile_picked_gatv_none_e_kernel(tc, xT, w1_words, w1_scales, score, offs, pos1, pos2, pos3, out):
@@ -51,19 +51,19 @@ def tile_picked_gatv_none_e_kernel(tc, xT, w1_words, w1_scales, score, offs, pos
         ident = keep.tile([P, P], F32, name="ident")
         planes = [keep.tile([P, T], F32, name="plane%d" % j) for j in range(4 * PASSES)]
 
-        make_identity(nc, ident[:])
         nc.gpsimd.memset(w_scales[:].rearrange("p z n -> p (z n)").bitcast(I32), 0)
-        nc.sync.dma_start(scores[:, :, 0:PER], score[:, 0, :].rearrange("d (p j) -> p d j", j=PER))
-        for j in range(4 * PASSES):
-            nc.sync.dma_start(planes[j][:], x_rows[j // 4, j % 4])
-            if j == 0:
-                nc.sync.dma_start(offs_t[:], offs)
-        nc.sync.dma_start(w_words[:], w1_words.rearrange("z p n -> p z n"))
+        make_identity(nc, ident[:])
+        nc.sync.dma_start(planes[0][:], x_rows[0, 0])
+        nc.scalar.dma_start(scores[:, :, 0:PER], score[:, 0, :].rearrange("d (p j) -> p d j", j=PER))
+        nc.sync.dma_start(offs_t[:], offs)
         for q in range(4):
-            nc.sync.dma_start(
+            nc.scalar.dma_start(
                 w_scales[32 * q : 32 * q + 4, :, :].bitcast(I32),
                 w1_scales[:, 4 * q : 4 * q + 4, :].rearrange("z r n -> r z n").bitcast(I32),
             )
+        for j in range(1, 4 * PASSES):
+            nc.sync.dma_start(planes[j][:], x_rows[j // 4, j % 4])
+        nc.sync.dma_start(w_words[:], w1_words.rearrange("z p n -> p z n"))
         for tile, src in zip(pos_t, (pos1, pos2, pos3)):
             nc.sync.dma_start(tile[:], src)
 
@@ -86,6 +86,12 @@ def tile_picked_gatv_none_e_kernel(tc, xT, w1_words, w1_scales, score, offs, pos
             for j in range(PER):
                 nc.tensor.transpose(spread[:, j * P : (j + 1) * P], weight[:, j, d : d + 1].to_broadcast([P, P]), ident[:])
             weight_rows.append(spread[:].rearrange("q (j p) -> q p j", j=PER))
+
+        first_rows = []
+        for d in range(1):
+            row = keep.tile([P, UNITS[0][2]], F32, name="first_row%d" % d)
+            nc.vector.tensor_copy(row[:].rearrange("q (p j) -> q p j", j=PER), weight_rows[d][:, 0 : UNITS[0][2] // PER, :])
+            first_rows.append(row)
 
         count = len(SLICES)
         acc = [[bank(D + len(BANKS[0]) * b + g) for g in range(len(BANKS[b]))] for b in range(BLOCKS)]
@@ -113,10 +119,11 @@ def tile_picked_gatv_none_e_kernel(tc, xT, w1_words, w1_scales, score, offs, pos
 
             for t0, width in GROUPS[z]:
                 tags = ["picked%d_%d_%d" % (z, t0, i) for i in range(len(PIECES))]
-                if z == 1 and t0 == 0:
-                    tags[0] = "woven0_%d" % (count - 1)
-                if z == 1 and t0 == 2:
-                    tags[0] = "picked1_0_%d" % (len(PIECES) - 1)
+                for i in VECTOR_PIECES[4 * z + t0]:
+                    if z == 1 and t0 == 0:
+                        tags[i] = "woven0_%d" % (count - 1 - i)
+                    if z == 1 and t0 == 2:
+                        tags[i] = "picked1_0_%d" % (len(PIECES) - 1 - i)
                 picked = [keep.tile([P, width, n], BF16, name="picked%d_%d_%d" % (z, t0, i), tag=tags[i], align_bytes=64) for i, (s, c0, n) in enumerate(PIECES)]
                 for e in range(width):
                     j = 4 * z + t0 + e
@@ -147,32 +154,49 @@ def tile_picked_gatv_none_e_kernel(tc, xT, w1_words, w1_scales, score, offs, pos
             else:
                 nc.vector.tensor_copy(y[b][:, j0 : j0 + n], acc[b][g][:, 0:n])
 
-        held = None
-        for b, v0, n, on_vector, pool_adds in UNITS:
-            terms = []
-            for d in range(D):
-                name = "%d_%d_%d" % (b, v0, d)
-                looked_up = y[b][:].indirect(pos_t[d][:, v0 // 16 : (v0 + n) // 16])
-                fetched = keep.tile([P, n], F32, name="fetched" + name, tag=held if d < on_vector and held else "fetched" + name)
-                if d == 1:
-                    held = "fetched" + name
-                term = keep.tile([P, n], F32, name="term" + name)
-                if d < on_vector:
-                    nc.vector.tensor_copy(fetched[:], looked_up)
-                else:
-                    nc.scalar.activation(fetched[:], looked_up, ACT.Copy)
-                nc.vector.tensor_tensor(
-                    term[:].rearrange("q (p j) -> q p j", j=PER),
-                    fetched[:].rearrange("q (p j) -> q p j", j=PER),
-                    weight_rows[d][:, v0 // PER : (v0 + n) // PER, :],
-                    ALU.mult,
-                )
-                terms.append(term)
-                if d == 1:
-                    partial = keep.tile([P, n], F32, name="partial%d_%d" % (b, v0))
-                    adder = nc.gpsimd if pool_adds > 0 else nc.vector
-                    adder.tensor_tensor(partial[:], terms[0][:], terms[1][:], ALU.add)
-            result = keep.tile([P, n], F32, name="result%d_%d" % (b, v0))
-            adder = nc.gpsimd if pool_adds > 1 else nc.vector
-            adder.tensor_tensor(result[:], partial[:], terms[2][:], ALU.add)
+        def look_up(unit, d, c0, c1):
+            b, v0 = UNITS[unit][0:2]
+            return y[b][:].indirect(pos_t[d][:, (v0 + c0) // 16 : (v0 + c1) // 16])
+
+        def weigh(unit, d):
+            b, v0, n = UNITS[unit][0:3]
+            term = keep.tile([P, n], F32, name="term%d_%d" % (unit, d))
+            nc.vector.tensor_tensor(
+                term[:].rearrange("q (p j) -> q p j", j=PER),
+                fetched[unit][d][:].rearrange("q (p j) -> q p j", j=PER),
+                weight_rows[d][:, v0 // PER : (v0 + n) // PER, :],
+                ALU.mult,
+            )
+            return term
+
+        def fetch_first(unit):
+            n, on_vector = UNITS[unit][2:4]
+            fetched[unit][0] = keep.tile([P, n], F32, name="fetched%d_0" % unit, tag="first_row0")
+            nc.vector.tensor_copy(fetched[unit][0][:, 0:on_vector], look_up(unit, 0, 0, on_vector))
+
+        fetched = [[None] * D for unit in UNITS]
+        for unit, (b, v0, n, on_vector, pool_adds) in enumerate(UNITS):
+            last = unit == len(UNITS) - 1
+            if unit > 0 and on_vector < n:
+                nc.scalar.activation(fetched[unit][0][:, on_vector:n], look_up(unit, 0, on_vector, n), ACT.Copy)
+            for d in range(1, D):
+                fetched[unit][d] = keep.tile([P, n], F32, name="fetched%d_%d" % (unit, d), tag="fetched%d_%d" % (unit % 2, d))
+                nc.scalar.activation(fetched[unit][d][:], look_up(unit, d, 0, n), ACT.Copy)
+            if unit == 0:
+                terms = [keep.tile([P, n], F32, name="term0_0")]
+                nc.vector.tensor_tensor(terms[0][:], look_up(0, 0, 0, n), first_rows[0][:], ALU.mult)
+                terms.append(weigh(0, 1))
+            else:
+                terms = [weigh(unit, 0), weigh(unit, 1)]
+            partial = keep.tile([P, n], F32, name="partial%d" % unit)
+            result = keep.tile([P, n], F32, name="result%d" % unit)
+            if last:
+                terms.append(weigh(unit, 2))
+                nc.vector.tensor_tensor(partial[:], terms[0][:], terms[1][:], ALU.add)
+                nc.vector.tensor_tensor(result[:], partial[:], terms[2][:], ALU.add)
+            else:
+                nc.gpsimd.tensor_tensor(partial[:], terms[0][:], terms[1][:], ALU.add)
+                fetch_first(unit + 1)
+                terms.append(weigh(unit, 2))
+                nc.gpsimd.tensor_tensor(result[:], partial[:], terms[2][:], ALU.add)
             nc.sync.dma_start(out[b * P : (b + 1) * P, v0 : v0 + n], result[:])

@@ -27,8 +27,8 @@ PER = V // P
 SLICES = [(0, 256), (256, 256), (512, 256), (768, 128), (896, 128)]
 PIECES = [(0, 0, 128), (0, 128, 128), (1, 0, 256), (2, 0, 256), (3, 0, 128), (4, 0, 128)]
 BANKS = [[[0, 1], [2, 3], [4]], [[0, 1], [2, 3, 4]]]
-GROUPS = [[(0, 4)], [(0, 2), (2, 2)]]
-VECTOR_PIECES = [[0, 1, 2], [0, 1, 2], [0, 1, 2], [0, 1], [0, 1], [0, 1], [0, 1, 2], [0]]
+GROUPS = [[(0, 2), (2, 2)], [(0, 2), (2, 2)]]
+VECTOR_PIECES = [[0, 1, 2], [0, 1, 2], [0, 1], [0, 1], [0, 1], [0, 1], [0, 1, 2], [0]]
 UNITS = ((0, 0, 256, 0, 2), (0, 256, 256, 256, 2), (1, 0, 256, 256, 2), (1, 256, 256, 128, 0))
 
 
@@ -95,6 +95,21 @@ def tile_picked_gatv_none_e_kernel(tc, xT, w1_words, w1_scales, score, offs, pos
 
         count = len(SLICES)
         acc = [[bank(D + len(BANKS[0]) * b + g) for g in range(len(BANKS[b]))] for b in range(BLOCKS)]
+        quantised = []
+
+        def multiply(b, z, s, words, plane):
+            g = [s in group for group in BANKS[b]].index(True)
+            c0 = SLICES[s][0] - SLICES[BANKS[b][g][0]][0]
+            nc.tensor.matmul_mx(
+                out=acc[b][g][:, c0 : c0 + SLICES[s][1]],
+                lhsT=w_words[:, z, 2 * P * b : 2 * P * (b + 1)].bitcast(FP4X4),
+                lhsT_scale=w_scales[:, z, P * b : P * (b + 1)],
+                rhs=words[:].bitcast(FP8X4),
+                rhs_scale=plane[:],
+                start=(z == 0 and s == BANKS[b][g][0]),
+                stop=(z == PASSES - 1 and s == BANKS[b][g][-1]),
+            )
+
         for z in range(PASSES):
             woven = [keep.tile([P, n, 4], BF16, name="woven%d_%d" % (z, s), align_bytes=64) for s, (j0, n) in enumerate(SLICES)]
             codes = [keep.tile([P, n], U32, name="codes%d_%d" % (z, s), align_bytes=64) for s, (j0, n) in enumerate(SLICES)]
@@ -104,26 +119,16 @@ def tile_picked_gatv_none_e_kernel(tc, xT, w1_words, w1_scales, score, offs, pos
                 nc.vector.quantize_mx(
                     out=codes[s][:].bitcast(FP8X4), scales=scales[s][:], in_=woven[s][:].rearrange("p n t -> p (n t)")
                 )
-                for b in range(BLOCKS):
-                    g = [s in group for group in BANKS[b]].index(True)
-                    c0 = SLICES[s][0] - SLICES[BANKS[b][g][0]][0]
-                    nc.tensor.matmul_mx(
-                        out=acc[b][g][:, c0 : c0 + SLICES[s][1]],
-                        lhsT=w_words[:, z, 2 * P * b : 2 * P * (b + 1)].bitcast(FP4X4),
-                        lhsT_scale=w_scales[:, z, P * b : P * (b + 1)],
-                        rhs=codes[s][:].bitcast(FP8X4),
-                        rhs_scale=scales[s][:],
-                        start=(z == 0 and s == BANKS[b][g][0]),
-                        stop=(z == PASSES - 1 and s == BANKS[b][g][-1]),
-                    )
+                multiply(0, z, s, codes[s], scales[s])
+                quantised.append((z, s, codes[s], scales[s]))
 
             for t0, width in GROUPS[z]:
                 tags = ["picked%d_%d_%d" % (z, t0, i) for i in range(len(PIECES))]
                 for i in VECTOR_PIECES[4 * z + t0]:
                     if z == 1 and t0 == 0:
                         tags[i] = "woven0_%d" % (count - 1 - i)
-                    if z == 1 and t0 == 2:
-                        tags[i] = "picked1_0_%d" % (len(PIECES) - 1 - i)
+                    if t0 == 2:
+                        tags[i] = "picked%d_0_%d" % (z, len(PIECES) - 1 - i)
                 picked = [keep.tile([P, width, n], BF16, name="picked%d_%d_%d" % (z, t0, i), tag=tags[i], align_bytes=64) for i, (s, c0, n) in enumerate(PIECES)]
                 for e in range(width):
                     j = 4 * z + t0 + e
@@ -136,23 +141,26 @@ def tile_picked_gatv_none_e_kernel(tc, xT, w1_words, w1_scales, score, offs, pos
                             nc.scalar.activation(picked[i][:, e, :], looked_up, ACT.Copy)
                 done = 0
                 for i, (s, c0, n) in enumerate(PIECES):
-                    nc.vector.tensor_copy(woven[s][:, c0 : c0 + n, t0 : t0 + width], picked[i][:].rearrange("p e n -> p n e"))
+                    if (z, t0, i) == (1, 2, len(PIECES) - 1):
+                        nc.scalar.copy(woven[s][:, c0 : c0 + n, t0 : t0 + width], picked[i][:].rearrange("p e n -> p n e"))
+                    else:
+                        nc.vector.tensor_copy(woven[s][:, c0 : c0 + n, t0 : t0 + width], picked[i][:].rearrange("p e n -> p n e"))
                     if t0 + width == 4 and s > done:
                         finish(done)
                         done = done + 1
             finish(count - 1)
+        for z, s, words, plane in quantised:
+            multiply(1, z, s, words, plane)
 
         y = [
             keep.tile([P, S], F32, name="y0", align_bytes=64),
             keep.tile([P, S], F32, name="y1", tag="woven1_%d" % (count - 1), align_bytes=64),
         ]
-        for b, g, engine in ((0, 0, "scalar"), (0, 1, "scalar"), (0, 2, "scalar"), (1, 0, "vector"), (1, 1, "vector")):
-            j0 = SLICES[BANKS[b][g][0]][0]
-            n = sum(SLICES[s][1] for s in BANKS[b][g])
-            if engine == "scalar":
-                nc.scalar.copy(y[b][:, j0 : j0 + n], acc[b][g][:, 0:n])
-            else:
-                nc.vector.tensor_copy(y[b][:, j0 : j0 + n], acc[b][g][:, 0:n])
+        nc.scalar.copy(y[0][:, 0:512], acc[0][0][:])
+        nc.scalar.copy(y[0][:, 512:896], acc[0][1][:, 0:384])
+        nc.vector.tensor_copy(y[1][:, 0:512], acc[1][0][:])
+        nc.vector.tensor_copy(y[0][:, 896:1024], acc[0][2][:, 0:128])
+        nc.vector.tensor_copy(y[1][:, 512:640], acc[1][1][:, 0:128])
 
         def look_up(unit, d, c0, c1):
             b, v0 = UNITS[unit][0:2]
@@ -186,6 +194,7 @@ def tile_picked_gatv_none_e_kernel(tc, xT, w1_words, w1_scales, score, offs, pos
                 terms = [keep.tile([P, n], F32, name="term0_0")]
                 nc.vector.tensor_tensor(terms[0][:], look_up(0, 0, 0, n), first_rows[0][:], ALU.mult)
                 terms.append(weigh(0, 1))
+                nc.vector.tensor_copy(y[1][:, 640:1024], acc[1][1][:, 128:512])
             else:
                 terms = [weigh(unit, 0), weigh(unit, 1)]
             partial = keep.tile([P, n], F32, name="partial%d" % unit)

@@ -25,11 +25,11 @@ BLOCKS = N // P
 BANK = 512
 PER = V // P
 SLICES = [(0, 256), (256, 256), (512, 256), (768, 128), (896, 128)]
-PIECES = [(0, 0, 128), (0, 128, 128), (1, 0, 256), (2, 0, 256), (3, 0, 128), (4, 0, 128)]
+PIECES = [(0, 0, 256), (1, 0, 256), (2, 0, 256), (3, 0, 128), (4, 0, 128)]
 BANKS = [[[0, 1], [2, 3], [4]], [[0, 1], [2, 3, 4]]]
 GROUPS = [[(0, 2), (2, 2)], [(0, 2), (2, 2)]]
-VECTOR_PIECES = [[0, 1, 2], [0, 1, 2], [0, 1], [0, 1], [0, 1], [0, 1], [0, 1, 2], [0]]
-UNITS = ((0, 0, 256, 0, 2), (0, 256, 256, 256, 2), (1, 0, 256, 256, 2), (1, 256, 256, 128, 0))
+VECTOR_PIECES = [[0, 1], [0, 1], [0], [0], [0], [0], [0, 1], [0]]
+UNITS = ((0, 0, 256, 0, 2), (0, 256, 256, 256, 2), (1, 0, 256, 256, 2), (1, 256, 256, 256, 0))
 
 
 def tile_picked_gatv_none_e_kernel(tc, xT, w1_words, w1_scales, score, offs, pos1, pos2, pos3, out):
@@ -129,19 +129,26 @@ def tile_picked_gatv_none_e_kernel(tc, xT, w1_words, w1_scales, score, offs, pos
                         tags[i] = "woven0_%d" % (count - 1 - i)
                     if t0 == 2:
                         tags[i] = "picked%d_0_%d" % (z, len(PIECES) - 1 - i)
-                picked = [keep.tile([P, width, n], BF16, name="picked%d_%d_%d" % (z, t0, i), tag=tags[i], align_bytes=64) for i, (s, c0, n) in enumerate(PIECES)]
+                picked = [
+                    None if (z, t0, i) == (1, 2, 0) else keep.tile([P, width, n], BF16, name="picked%d_%d_%d" % (z, t0, i), tag=tags[i], align_bytes=64)
+                    for i, (s, c0, n) in enumerate(PIECES)
+                ]
                 for e in range(width):
                     j = 4 * z + t0 + e
                     for i, (s, c0, n) in enumerate(PIECES):
                         j0 = SLICES[s][0] + c0
                         looked_up = planes[j][:].indirect(offs_t[:, j0 // 16 : (j0 + n) // 16])
-                        if i in VECTOR_PIECES[j]:
+                        if (z, t0, i) == (1, 2, 0):
+                            nc.vector.tensor_copy(woven[s][:, :, t0 + e], looked_up)
+                        elif i in VECTOR_PIECES[j]:
                             nc.vector.tensor_copy(picked[i][:, e, :], looked_up)
                         else:
                             nc.scalar.activation(picked[i][:, e, :], looked_up, ACT.Copy)
                 done = 0
                 for i, (s, c0, n) in enumerate(PIECES):
-                    if (z, t0, i) == (1, 2, len(PIECES) - 1):
+                    if (z, t0, i) == (1, 2, 0):
+                        continue
+                    if (z, t0) == (1, 2) and i >= len(PIECES) - 2:
                         nc.scalar.copy(woven[s][:, c0 : c0 + n, t0 : t0 + width], picked[i][:].rearrange("p e n -> p n e"))
                     else:
                         nc.vector.tensor_copy(woven[s][:, c0 : c0 + n, t0 : t0 + width], picked[i][:].rearrange("p e n -> p n e"))
@@ -160,7 +167,6 @@ def tile_picked_gatv_none_e_kernel(tc, xT, w1_words, w1_scales, score, offs, pos
         nc.scalar.copy(y[0][:, 512:896], acc[0][1][:, 0:384])
         nc.vector.tensor_copy(y[1][:, 0:512], acc[1][0][:])
         nc.vector.tensor_copy(y[0][:, 896:1024], acc[0][2][:, 0:128])
-        nc.vector.tensor_copy(y[1][:, 512:640], acc[1][1][:, 0:128])
 
         def look_up(unit, d, c0, c1):
             b, v0 = UNITS[unit][0:2]
@@ -180,32 +186,45 @@ def tile_picked_gatv_none_e_kernel(tc, xT, w1_words, w1_scales, score, offs, pos
         def fetch_first(unit):
             n, on_vector = UNITS[unit][2:4]
             fetched[unit][0] = keep.tile([P, n], F32, name="fetched%d_0" % unit, tag="first_row0")
-            nc.vector.tensor_copy(fetched[unit][0][:, 0:on_vector], look_up(unit, 0, 0, on_vector))
+            if on_vector > 0:
+                nc.vector.tensor_copy(fetched[unit][0][:, 0:on_vector], look_up(unit, 0, 0, on_vector))
 
         fetched = [[None] * D for unit in UNITS]
         for unit, (b, v0, n, on_vector, pool_adds) in enumerate(UNITS):
             last = unit == len(UNITS) - 1
             if unit > 0 and on_vector < n:
                 nc.scalar.activation(fetched[unit][0][:, on_vector:n], look_up(unit, 0, on_vector, n), ACT.Copy)
-            for d in range(1, D):
+            for d in range(1, D - 1 if last else D):
                 fetched[unit][d] = keep.tile([P, n], F32, name="fetched%d_%d" % (unit, d), tag="fetched%d_%d" % (unit % 2, d))
                 nc.scalar.activation(fetched[unit][d][:], look_up(unit, d, 0, n), ACT.Copy)
             if unit == 0:
                 terms = [keep.tile([P, n], F32, name="term0_0")]
                 nc.vector.tensor_tensor(terms[0][:], look_up(0, 0, 0, n), first_rows[0][:], ALU.mult)
                 terms.append(weigh(0, 1))
-                nc.vector.tensor_copy(y[1][:, 640:1024], acc[1][1][:, 128:512])
+                nc.scalar.copy(y[1][:, 512:1024], acc[1][1][:])
             else:
                 terms = [weigh(unit, 0), weigh(unit, 1)]
             partial = keep.tile([P, n], F32, name="partial%d" % unit)
-            result = keep.tile([P, n], F32, name="result%d" % unit)
             if last:
-                terms.append(weigh(unit, 2))
                 nc.vector.tensor_tensor(partial[:], terms[0][:], terms[1][:], ALU.add)
-                nc.vector.tensor_tensor(result[:], partial[:], terms[2][:], ALU.add)
+                half = n // 2
+                for c0 in (0, half):
+                    piece = keep.tile([P, half], F32, name="piece%d" % c0)
+                    term = keep.tile([P, half], F32, name="last_term%d" % c0)
+                    result = keep.tile([P, half], F32, name="last_result%d" % c0)
+                    nc.scalar.activation(piece[:], look_up(unit, D - 1, c0, c0 + half), ACT.Copy)
+                    nc.vector.tensor_tensor(
+                        term[:].rearrange("q (p j) -> q p j", j=PER),
+                        piece[:].rearrange("q (p j) -> q p j", j=PER),
+                        weight_rows[D - 1][:, (v0 + c0) // PER : (v0 + c0 + half) // PER, :],
+                        ALU.mult,
+                    )
+                    nc.vector.tensor_tensor(result[:], partial[:, c0 : c0 + half], term[:], ALU.add)
+                    nc.sync.dma_start(out[b * P : (b + 1) * P, v0 + c0 : v0 + c0 + half], result[:])
             else:
+                result = keep.tile([P, n], F32, name="result%d" % unit)
                 nc.gpsimd.tensor_tensor(partial[:], terms[0][:], terms[1][:], ALU.add)
                 fetch_first(unit + 1)
                 terms.append(weigh(unit, 2))
                 nc.gpsimd.tensor_tensor(result[:], partial[:], terms[2][:], ALU.add)
-            nc.sync.dma_start(out[b * P : (b + 1) * P, v0 : v0 + n], result[:])
+                nc.sync.dma_start(out[b * P : (b + 1) * P, v0 : v0 + n], result[:])

@@ -24,12 +24,11 @@ PASSES = K // 512
 BLOCKS = N // P
 BANK = 512
 PER = V // P
-SLICES = [(0, 256), (256, 256), (512, 256), (768, 128), (896, 128)]
-PIECES = [(0, 0, 256), (1, 0, 256), (2, 0, 256), (3, 0, 128), (4, 0, 128)]
-BANKS = [[[0, 1], [2, 3], [4]], [[0, 1], [2, 3, 4]]]
-GROUPS = [[(0, 2), (2, 2)], [(0, 2), (2, 2)]]
-VECTOR_PIECES = [[0, 1], [0, 1], [0], [0], [0], [0], [0, 1], [0]]
-UNITS = ((0, 0, 256, 0, 2), (0, 256, 256, 256, 2), (1, 0, 256, 256, 2), (1, 256, 256, 256, 0))
+SLICES = [[(0, 512), (512, 512)], [(0, 256), (256, 256), (512, 256), (768, 128), (896, 128)]]
+PIECES = [[(0, 0, 256), (0, 256, 256), (1, 0, 256), (1, 256, 256)], [(0, 0, 256), (1, 0, 256), (2, 0, 256), (3, 0, 128), (4, 0, 128)]]
+VECTOR_PIECES = [[0, 1], [0, 1], [0], [0], [0], [0], [0], [0]]
+UNIT = 256
+FUSED = 512
 
 
 def tile_picked_gatv_none_e_kernel(tc, xT, w1_words, w1_scales, score, offs, pos1, pos2, pos3, out):
@@ -87,56 +86,60 @@ def tile_picked_gatv_none_e_kernel(tc, xT, w1_words, w1_scales, score, offs, pos
                 nc.tensor.transpose(spread[:, j * P : (j + 1) * P], weight[:, j, d : d + 1].to_broadcast([P, P]), ident[:])
             weight_rows.append(spread[:].rearrange("q (j p) -> q p j", j=PER))
 
-        first_rows = []
-        for d in range(1):
-            row = keep.tile([P, UNITS[0][2]], F32, name="first_row%d" % d)
-            nc.vector.tensor_copy(row[:].rearrange("q (p j) -> q p j", j=PER), weight_rows[d][:, 0 : UNITS[0][2] // PER, :])
-            first_rows.append(row)
+        first_rows = keep.tile([P, FUSED], F32, name="first_rows")
+        nc.vector.tensor_copy(first_rows[:].rearrange("q (p j) -> q p j", j=PER), weight_rows[0][:, 0 : FUSED // PER, :])
 
-        count = len(SLICES)
-        acc = [[bank(D + len(BANKS[0]) * b + g) for g in range(len(BANKS[b]))] for b in range(BLOCKS)]
-        quantised = []
+        codes, scales = [], []
+        front = [bank(D + i) for i in range(4)]
+        back = [bank(D + 4), None]
 
-        def multiply(b, z, s, words, plane):
-            g = [s in group for group in BANKS[b]].index(True)
-            c0 = SLICES[s][0] - SLICES[BANKS[b][g][0]][0]
+        def multiply(acc, b, z, j0, n, base, start, stop):
+            s = [lo <= j0 < lo + width for lo, width in SLICES[z]].index(True)
+            c0 = j0 - SLICES[z][s][0]
             nc.tensor.matmul_mx(
-                out=acc[b][g][:, c0 : c0 + SLICES[s][1]],
+                out=acc[:, j0 - base : j0 - base + n],
                 lhsT=w_words[:, z, 2 * P * b : 2 * P * (b + 1)].bitcast(FP4X4),
                 lhsT_scale=w_scales[:, z, P * b : P * (b + 1)],
-                rhs=words[:].bitcast(FP8X4),
-                rhs_scale=plane[:],
-                start=(z == 0 and s == BANKS[b][g][0]),
-                stop=(z == PASSES - 1 and s == BANKS[b][g][-1]),
+                rhs=codes[z][s][:, c0 : c0 + n].bitcast(FP8X4),
+                rhs_scale=scales[z][s][:, c0 : c0 + n],
+                start=start,
+                stop=stop,
             )
 
         for z in range(PASSES):
-            woven = [keep.tile([P, n, 4], BF16, name="woven%d_%d" % (z, s), align_bytes=64) for s, (j0, n) in enumerate(SLICES)]
-            codes = [keep.tile([P, n], U32, name="codes%d_%d" % (z, s), align_bytes=64) for s, (j0, n) in enumerate(SLICES)]
-            scales = [keep.tile([P, n], U8, name="scales%d_%d" % (z, s), align_bytes=64) for s, (j0, n) in enumerate(SLICES)]
+            count = len(SLICES[z])
+            pieces = PIECES[z]
+            woven = [keep.tile([P, n, 4], BF16, name="woven%d_%d" % (z, s), align_bytes=64) for s, (j0, n) in enumerate(SLICES[z])]
+            codes.append([keep.tile([P, n], U32, name="codes%d_%d" % (z, s), align_bytes=64) for s, (j0, n) in enumerate(SLICES[z])])
+            scales.append([keep.tile([P, n], U8, name="scales%d_%d" % (z, s), align_bytes=64) for s, (j0, n) in enumerate(SLICES[z])])
 
             def finish(s):
                 nc.vector.quantize_mx(
-                    out=codes[s][:].bitcast(FP8X4), scales=scales[s][:], in_=woven[s][:].rearrange("p n t -> p (n t)")
+                    out=codes[z][s][:].bitcast(FP8X4), scales=scales[z][s][:], in_=woven[s][:].rearrange("p n t -> p (n t)")
                 )
-                multiply(0, z, s, codes[s], scales[s])
-                quantised.append((z, s, codes[s], scales[s]))
+                if z == 1:
+                    j0, n = SLICES[z][s]
+                    if s < 2:
+                        multiply(front[0], 0, 1, j0, n, 0, False, s == 1)
+                        multiply(back[0], 1, 1, j0, n, 0, False, s == 1)
+                    else:
+                        multiply(front[s - 1], 0, 1, j0, n, j0, False, True)
 
-            for t0, width in GROUPS[z]:
-                tags = ["picked%d_%d_%d" % (z, t0, i) for i in range(len(PIECES))]
+            for t0 in (0, 2):
+                tags = ["picked%d_%d_%d" % (z, t0, i) for i in range(len(pieces))]
                 for i in VECTOR_PIECES[4 * z + t0]:
                     if z == 1 and t0 == 0:
-                        tags[i] = "woven0_%d" % (count - 1 - i)
+                        tags[i] = "woven0_%d" % (len(SLICES[0]) - 1 - i)
                     if t0 == 2:
-                        tags[i] = "picked%d_0_%d" % (z, len(PIECES) - 1 - i)
+                        tags[i] = "picked%d_0_%d" % (z, len(pieces) - 1 - i)
                 picked = [
-                    None if (z, t0, i) == (1, 2, 0) else keep.tile([P, width, n], BF16, name="picked%d_%d_%d" % (z, t0, i), tag=tags[i], align_bytes=64)
-                    for i, (s, c0, n) in enumerate(PIECES)
+                    None if (z, t0, i) == (1, 2, 0) else keep.tile([P, 2, n], BF16, name="picked%d_%d_%d" % (z, t0, i), tag=tags[i], align_bytes=64)
+                    for i, (s, c0, n) in enumerate(pieces)
                 ]
-                for e in range(width):
+                for e in range(2):
                     j = 4 * z + t0 + e
-                    for i, (s, c0, n) in enumerate(PIECES):
-                        j0 = SLICES[s][0] + c0
+                    for i, (s, c0, n) in enumerate(pieces):
+                        j0 = SLICES[z][s][0] + c0
                         looked_up = planes[j][:].indirect(offs_t[:, j0 // 16 : (j0 + n) // 16])
                         if (z, t0, i) == (1, 2, 0):
                             nc.vector.tensor_copy(woven[s][:, :, t0 + e], looked_up)
@@ -145,86 +148,111 @@ def tile_picked_gatv_none_e_kernel(tc, xT, w1_words, w1_scales, score, offs, pos
                         else:
                             nc.scalar.activation(picked[i][:, e, :], looked_up, ACT.Copy)
                 done = 0
-                for i, (s, c0, n) in enumerate(PIECES):
+                for i, (s, c0, n) in enumerate(pieces):
                     if (z, t0, i) == (1, 2, 0):
                         continue
-                    if (z, t0) == (1, 2) and i >= len(PIECES) - 2:
-                        nc.scalar.copy(woven[s][:, c0 : c0 + n, t0 : t0 + width], picked[i][:].rearrange("p e n -> p n e"))
+                    if (z, t0) == (1, 2) and i >= len(pieces) - 2:
+                        nc.scalar.copy(woven[s][:, c0 : c0 + n, t0 : t0 + 2], picked[i][:].rearrange("p e n -> p n e"))
                     else:
-                        nc.vector.tensor_copy(woven[s][:, c0 : c0 + n, t0 : t0 + width], picked[i][:].rearrange("p e n -> p n e"))
-                    if t0 + width == 4 and s > done:
+                        nc.vector.tensor_copy(woven[s][:, c0 : c0 + n, t0 : t0 + 2], picked[i][:].rearrange("p e n -> p n e"))
+                    if t0 == 2 and s > done:
                         finish(done)
                         done = done + 1
             finish(count - 1)
-        for z, s, words, plane in quantised:
-            multiply(1, z, s, words, plane)
+            if z == 0:
+                multiply(front[0], 0, 0, 0, 512, 0, True, False)
+                for s in range(2, len(SLICES[1])):
+                    j0, n = SLICES[1][s]
+                    multiply(front[s - 1], 0, 0, j0, n, j0, True, False)
+                multiply(back[0], 1, 0, 0, 512, 0, True, False)
 
         y = [
             keep.tile([P, S], F32, name="y0", align_bytes=64),
-            keep.tile([P, S], F32, name="y1", tag="woven1_%d" % (count - 1), align_bytes=64),
+            keep.tile([P, S], F32, name="y1", tag="woven1_%d" % (len(SLICES[1]) - 1), align_bytes=64),
         ]
-        nc.scalar.copy(y[0][:, 0:512], acc[0][0][:])
-        nc.scalar.copy(y[0][:, 512:896], acc[0][1][:, 0:384])
-        nc.vector.tensor_copy(y[1][:, 0:512], acc[1][0][:])
-        nc.vector.tensor_copy(y[0][:, 896:1024], acc[0][2][:, 0:128])
+        nc.scalar.copy(y[0][:, 0:512], front[0][:])
+        nc.vector.tensor_copy(y[0][:, 512:768], front[1][:, 0:256])
+        nc.scalar.copy(y[0][:, 768:896], front[2][:, 0:128])
+        nc.scalar.copy(y[0][:, 896:1024], front[3][:, 0:128])
+        nc.vector.tensor_copy(y[1][:, 0:512], back[0][:])
+        back[1] = bank(D + 2)
+        multiply(back[1], 1, 0, 512, 512, 512, True, False)
+        for j0, n in SLICES[1][2:]:
+            multiply(back[1], 1, 1, j0, n, 512, False, j0 + n == S)
 
-        def look_up(unit, d, c0, c1):
-            b, v0 = UNITS[unit][0:2]
-            return y[b][:].indirect(pos_t[d][:, (v0 + c0) // 16 : (v0 + c1) // 16])
+        def look_up(b, d, v0, n):
+            return y[b][:].indirect(pos_t[d][:, v0 // 16 : (v0 + n) // 16])
 
-        def weigh(unit, d):
-            b, v0, n = UNITS[unit][0:3]
-            term = keep.tile([P, n], F32, name="term%d_%d" % (unit, d))
+        def fresh(kind, b, d, v0, n, tag=None):
+            name = "%s%d_%d_%d" % (kind, b, d, v0)
+            return keep.tile([P, n], F32, name=name, tag=tag or name)
+
+        def fetch(engine, b, d, v0, n, tag=None):
+            got = fresh("fetched", b, d, v0, n, tag)
+            if engine == "scalar":
+                nc.scalar.activation(got[:], look_up(b, d, v0, n), ACT.Copy)
+            else:
+                nc.vector.tensor_copy(got[:], look_up(b, d, v0, n))
+            return got
+
+        def fused(b, v0, n, tag=None, into=None):
+            term = fresh("term", b, 0, v0, n, tag) if into is None else into
+            nc.vector.tensor_tensor(term[:], look_up(b, 0, v0, n), first_rows[:, v0 : v0 + n], ALU.mult)
+            return term
+
+        def weigh(got, b, d, v0, n, tag=None, into=None):
+            term = fresh("term", b, d, v0, n, tag) if into is None else into
             nc.vector.tensor_tensor(
                 term[:].rearrange("q (p j) -> q p j", j=PER),
-                fetched[unit][d][:].rearrange("q (p j) -> q p j", j=PER),
+                got.rearrange("q (p j) -> q p j", j=PER),
                 weight_rows[d][:, v0 // PER : (v0 + n) // PER, :],
                 ALU.mult,
             )
             return term
 
-        def fetch_first(unit):
-            n, on_vector = UNITS[unit][2:4]
-            fetched[unit][0] = keep.tile([P, n], F32, name="fetched%d_0" % unit, tag="first_row0")
-            if on_vector > 0:
-                nc.vector.tensor_copy(fetched[unit][0][:, 0:on_vector], look_up(unit, 0, 0, on_vector))
+        def add(engine, kind, one, other, b, v0, n, tag=None):
+            total = fresh(kind, b, 0, v0, n, tag)
+            engine.tensor_tensor(total[:], one, other, ALU.add)
+            return total
 
-        fetched = [[None] * D for unit in UNITS]
-        for unit, (b, v0, n, on_vector, pool_adds) in enumerate(UNITS):
-            last = unit == len(UNITS) - 1
-            if unit > 0 and on_vector < n:
-                nc.scalar.activation(fetched[unit][0][:, on_vector:n], look_up(unit, 0, on_vector, n), ACT.Copy)
-            for d in range(1, D - 1 if last else D):
-                fetched[unit][d] = keep.tile([P, n], F32, name="fetched%d_%d" % (unit, d), tag="fetched%d_%d" % (unit % 2, d))
-                nc.scalar.activation(fetched[unit][d][:], look_up(unit, d, 0, n), ACT.Copy)
-            if unit == 0:
-                terms = [keep.tile([P, n], F32, name="term0_0")]
-                nc.vector.tensor_tensor(terms[0][:], look_up(0, 0, 0, n), first_rows[0][:], ALU.mult)
-                terms.append(weigh(0, 1))
-                nc.scalar.copy(y[1][:, 512:1024], acc[1][1][:])
-            else:
-                terms = [weigh(unit, 0), weigh(unit, 1)]
-            partial = keep.tile([P, n], F32, name="partial%d" % unit)
-            if last:
-                nc.vector.tensor_tensor(partial[:], terms[0][:], terms[1][:], ALU.add)
-                half = n // 2
-                for c0 in (0, half):
-                    piece = keep.tile([P, half], F32, name="piece%d" % c0)
-                    term = keep.tile([P, half], F32, name="last_term%d" % c0)
-                    result = keep.tile([P, half], F32, name="last_result%d" % c0)
-                    nc.scalar.activation(piece[:], look_up(unit, D - 1, c0, c0 + half), ACT.Copy)
-                    nc.vector.tensor_tensor(
-                        term[:].rearrange("q (p j) -> q p j", j=PER),
-                        piece[:].rearrange("q (p j) -> q p j", j=PER),
-                        weight_rows[D - 1][:, (v0 + c0) // PER : (v0 + c0 + half) // PER, :],
-                        ALU.mult,
-                    )
-                    nc.vector.tensor_tensor(result[:], partial[:, c0 : c0 + half], term[:], ALU.add)
-                    nc.sync.dma_start(out[b * P : (b + 1) * P, v0 + c0 : v0 + c0 + half], result[:])
-            else:
-                result = keep.tile([P, n], F32, name="result%d" % unit)
-                nc.gpsimd.tensor_tensor(partial[:], terms[0][:], terms[1][:], ALU.add)
-                fetch_first(unit + 1)
-                terms.append(weigh(unit, 2))
-                nc.gpsimd.tensor_tensor(result[:], partial[:], terms[2][:], ALU.add)
-                nc.sync.dma_start(out[b * P : (b + 1) * P, v0 : v0 + n], result[:])
+        def store(result, b, v0, n):
+            nc.sync.dma_start(out[b * P : (b + 1) * P, v0 : v0 + n], result[:])
+
+        n = UNIT
+        g01 = fetch("scalar", 0, 1, 0, n)
+        g11 = fetch("scalar", 0, 1, n, n)
+        nc.scalar.copy(y[1][:, 512:1024], back[1][:])
+        g02 = fetch("scalar", 0, 2, 0, n)
+        g20 = fetch("scalar", 1, 0, 0, n)
+        g21 = fetch("scalar", 1, 1, 0, n)
+        g31 = fetch("scalar", 1, 1, n, n)
+        g22 = fetch("scalar", 1, 2, 0, n)
+        g32 = [fetch("scalar", 1, 2, n + c0, n // 2) for c0 in (0, n // 2)]
+        t0 = fused(0, 0, FUSED)
+        partial = keep.tile([P, V], F32, name="partial0")
+        t2 = keep.tile([P, V], F32, name="third0")
+        t01 = weigh(g01[:], 0, 1, 0, n)
+        nc.gpsimd.tensor_tensor(partial[:, 0:n], t0[:, 0:n], t01[:], ALU.add)
+        t11 = weigh(g11[:], 0, 1, n, n)
+        nc.gpsimd.tensor_tensor(partial[:, n:V], t0[:, n:V], t11[:], ALU.add)
+        g12 = fetch("vector", 0, 2, n, n, tag="fetched0_1_0")
+        h = n // 2
+        g30 = [fetch("vector", 1, 0, n, h, tag="fetched0_1_256")]
+        weigh(g02[:], 0, 2, 0, n, into=t2[:, 0:n])
+        weigh(g12[:], 0, 2, n, n, into=t2[:, n:V])
+        g30.append(fetch("vector", 1, 0, n + h, h, tag="fetched0_2_0"))
+        store(add(nc.gpsimd, "result", partial[:], t2[:], 0, 0, V), 0, 0, V)
+        t20 = weigh(g20[:], 1, 0, 0, n)
+        t30 = keep.tile([P, n], F32, name="first3")
+        weigh(g30[0][:], 1, 0, n, h, into=t30[:, 0:h])
+        weigh(g30[1][:], 1, 0, n + h, h, into=t30[:, h:n])
+        t21 = weigh(g21[:], 1, 1, 0, n)
+        t31 = weigh(g31[:], 1, 1, n, n)
+        p2 = add(nc.vector, "partial", t20[:], t21[:], 1, 0, n)
+        p3 = add(nc.vector, "partial", t30[:], t31[:], 1, n, n)
+        t22 = weigh(g22[:], 1, 2, 0, n)
+        last = [weigh(g32[0][:], 1, 2, n, h)]
+        store(add(nc.vector, "result", p2[:], t22[:], 1, 0, n), 1, 0, n)
+        last.append(weigh(g32[1][:], 1, 2, n + h, h))
+        for i, c0 in enumerate((0, h)):
+            store(add(nc.vector, "result", p3[:, c0 : c0 + h], last[i][:], 1, n + c0, h), 1, n + c0, h)

@@ -45,7 +45,7 @@ def tile_picked_gatv_none_e_kernel(tc, xT, w1_words, w1_scales, score, offs, pos
         offs_t = lists.tile([P, S // 16], U16, name="offs_t")
         pos_t = [lists.tile([P, V // 16], U16, name="pos_t%d" % d) for d in range(D)]
         scores = keep.tile([P, D, 8], F32, name="scores")
-        w_words = keep.tile([P, PASSES, 2 * N], U8, name="w_words", align_bytes=64)
+        w_words = [keep.tile([P, 2 * N], U8, name="w_words%d" % z, align_bytes=64) for z in range(PASSES)]
         w_scales = keep.tile([P, PASSES, N], U8, name="w_scales", align_bytes=64)
         ident = keep.tile([P, P], F32, name="ident")
         planes = [keep.tile([P, T], F32, name="plane%d" % j) for j in range(4 * PASSES)]
@@ -62,7 +62,8 @@ def tile_picked_gatv_none_e_kernel(tc, xT, w1_words, w1_scales, score, offs, pos
             )
         for j in range(1, 4 * PASSES):
             nc.sync.dma_start(planes[j][:], x_rows[j // 4, j % 4])
-        nc.sync.dma_start(w_words[:], w1_words.rearrange("z p n -> p z n"))
+        for z in range(PASSES):
+            nc.sync.dma_start(w_words[z][:], w1_words[z])
         for tile, src in zip(pos_t, (pos1, pos2, pos3)):
             nc.sync.dma_start(tile[:], src)
 
@@ -98,7 +99,7 @@ def tile_picked_gatv_none_e_kernel(tc, xT, w1_words, w1_scales, score, offs, pos
             c0 = j0 - SLICES[z][s][0]
             nc.tensor.matmul_mx(
                 out=acc[:, j0 - base : j0 - base + n],
-                lhsT=w_words[:, z, 2 * P * b : 2 * P * (b + 1)].bitcast(FP4X4),
+                lhsT=w_words[z][:, 2 * P * b : 2 * P * (b + 1)].bitcast(FP4X4),
                 lhsT_scale=w_scales[:, z, P * b : P * (b + 1)],
                 rhs=codes[z][s][:, c0 : c0 + n].bitcast(FP8X4),
                 rhs_scale=scales[z][s][:, c0 : c0 + n],

@@ -84,11 +84,11 @@ def tile_picked_gatv_none_e_kernel(tc, xT, w1_words, w1_scales, score, offs, pos
         for d in range(D):
             spread = bank(d)
             for j in range(PER):
-                nc.tensor.transpose(spread[:, j * P : (j + 1) * P], weight[:, j, d : d + 1].to_broadcast([P, P]), ident[:])
-            weight_rows.append(spread[:].rearrange("q (j p) -> q p j", j=PER))
+                nc.tensor.transpose(spread[:, j : BANK : PER], weight[:, j, d : d + 1].to_broadcast([P, P]), ident[:])
+            weight_rows.append(spread)
 
         first_rows = keep.tile([P, FUSED], F32, name="first_rows")
-        nc.vector.tensor_copy(first_rows[:].rearrange("q (p j) -> q p j", j=PER), weight_rows[0][:, 0 : FUSED // PER, :])
+        nc.vector.tensor_copy(first_rows[:], weight_rows[0][:, 0:FUSED])
 
         codes, scales = [], []
         front = [bank(D + i) for i in range(4)]
@@ -203,12 +203,7 @@ def tile_picked_gatv_none_e_kernel(tc, xT, w1_words, w1_scales, score, offs, pos
 
         def weigh(got, b, d, v0, n, tag=None, into=None):
             term = fresh("term", b, d, v0, n, tag) if into is None else into
-            nc.vector.tensor_tensor(
-                term[:].rearrange("q (p j) -> q p j", j=PER),
-                got.rearrange("q (p j) -> q p j", j=PER),
-                weight_rows[d][:, v0 // PER : (v0 + n) // PER, :],
-                ALU.mult,
-            )
+            nc.vector.tensor_tensor(term[:], got, weight_rows[d][:, v0 : v0 + n], ALU.mult)
             return term
 
         def add(engine, kind, one, other, b, v0, n, tag=None):

@@ -221,8 +221,8 @@ def tile_picked_gatv_none_e_kernel(tc, xT, w1_words, w1_scales, score, offs, pos
         g02 = fetch("scalar", 0, 2, 0, n)
         g20 = fetch("scalar", 1, 0, 0, n)
         g21 = fetch("scalar", 1, 1, 0, n)
-        g31 = fetch("scalar", 1, 1, n, n)
         g22 = fetch("scalar", 1, 2, 0, n)
+        g31 = fetch("scalar", 1, 1, n, n)
         g32 = [fetch("scalar", 1, 2, n + c0, n // 2) for c0 in (0, n // 2)]
         t0 = fused(0, 0, FUSED)
         partial = keep.tile([P, V], F32, name="partial0")
@@ -243,12 +243,12 @@ def tile_picked_gatv_none_e_kernel(tc, xT, w1_words, w1_scales, score, offs, pos
         weigh(g30[0][:], 1, 0, n, h, into=t30[:, 0:h])
         weigh(g30[1][:], 1, 0, n + h, h, into=t30[:, h:n])
         t21 = weigh(g21[:], 1, 1, 0, n)
-        t31 = weigh(g31[:], 1, 1, n, n)
-        p2 = add(nc.vector, "partial", t20[:], t21[:], 1, 0, n)
-        p3 = add(nc.vector, "partial", t30[:], t31[:], 1, n, n)
         t22 = weigh(g22[:], 1, 2, 0, n)
-        last = [weigh(g32[0][:], 1, 2, n, h)]
+        p2 = add(nc.vector, "partial", t20[:], t21[:], 1, 0, n)
+        t31 = weigh(g31[:], 1, 1, n, n)
         store(add(nc.vector, "result", p2[:], t22[:], 1, 0, n), 1, 0, n)
+        last = [weigh(g32[0][:], 1, 2, n, h)]
+        p3 = add(nc.vector, "partial", t30[:], t31[:], 1, n, n)
         last.append(weigh(g32[1][:], 1, 2, n + h, h))
         for i, c0 in enumerate((0, h)):
             store(add(nc.vector, "result", p3[:, c0 : c0 + h], last[i][:], 1, n + c0, h), 1, n + c0, h)

@@ -44,16 +44,18 @@ def tile_picked_gatv_none_e_kernel(tc, xT, w1_words, w1_scales, score, offs, pos
         x_rows = xT.rearrange("(z p t) c -> z t p c", p=P, t=4)
         offs_t = lists.tile([P, S // 16], U16, name="offs_t")
         pos_t = [lists.tile([P, V // 16], U16, name="pos_t%d" % d) for d in range(D)]
-        scores = keep.tile([P, D, 8], F32, name="scores")
+        raw = keep.tile([P, P], F32, name="raw", align_bytes=64)
+        scores = keep.tile([P, P], F32, name="scores", align_bytes=64)
         w_words = [keep.tile([P, 2 * N], U8, name="w_words%d" % z, align_bytes=64) for z in range(PASSES)]
         w_scales = keep.tile([P, PASSES, N], U8, name="w_scales", align_bytes=64)
         ident = keep.tile([P, P], F32, name="ident")
         planes = [keep.tile([P, T], F32, name="plane%d" % j) for j in range(4 * PASSES)]
 
+        nc.gpsimd.memset(raw[:], 0.0)
         nc.gpsimd.memset(w_scales[:].rearrange("p z n -> p (z n)").bitcast(I32), 0)
         make_identity(nc, ident[:])
         nc.sync.dma_start(planes[0][:], x_rows[0, 0])
-        nc.scalar.dma_start(scores[:, :, 0:PER], score[:, 0, :].rearrange("d (p j) -> p d j", j=PER))
+        nc.scalar.dma_start(raw[0:P:8, 0 : 32 * D].rearrange("s (d c) -> s d c", c=32), score[:, 0, :].rearrange("d (s c) -> s d c", c=32))
         nc.sync.dma_start(offs_t[:], offs)
         for q in range(4):
             nc.scalar.dma_start(
@@ -67,7 +69,8 @@ def tile_picked_gatv_none_e_kernel(tc, xT, w1_words, w1_scales, score, offs, pos
         for tile, src in zip(pos_t, (pos1, pos2, pos3)):
             nc.sync.dma_start(tile[:], src)
 
-        by_target = scores[:, :, 0:PER].rearrange("p d j -> p j d")
+        nc.vector.transpose(scores[:], raw[:])
+        by_target = scores[:].rearrange("p (d j e) -> p j d e", j=PER, e=8)[:, :, 0:D, 0]
         top = keep.tile([P, PER], F32, name="top")
         shifted = keep.tile([P, PER, D], F32, name="shifted")
         expd = keep.tile([P, PER, D], F32, name="expd")
@@ -84,7 +87,7 @@ def tile_picked_gatv_none_e_kernel(tc, xT, w1_words, w1_scales, score, offs, pos
         for d in range(D):
             spread = bank(d)
             for j in range(PER):
-                nc.tensor.transpose(spread[:, j : BANK : PER], weight[:, j, d : d + 1].to_broadcast([P, P]), ident[:])
+                nc.tensor.transpose(spread[:].rearrange("p (q s c) -> p s q c", q=4, c=32)[:, j], weight[:, j, d : d + 1].to_broadcast([P, P]), ident[:])
             weight_rows.append(spread)
 
         first_rows = keep.tile([P, FUSED], F32, name="first_rows")

@@ -25,7 +25,7 @@ BLOCKS = N // P
 BANK = 512
 PER = V // P
 SLICES = [[(0, 512), (512, 512)], [(0, 256), (256, 256), (512, 256), (768, 128), (896, 128)]]
-PIECES = [[(0, 0, 256), (0, 256, 256), (1, 0, 256), (1, 256, 256)], [(0, 0, 256), (1, 0, 256), (2, 0, 256), (3, 0, 128), (4, 0, 128)]]
+PIECES = [[(0, 0, 256), (0, 256, 256), (1, 0, 512)], [(0, 0, 256), (1, 0, 256), (2, 0, 256), (3, 0, 128), (4, 0, 128)]]
 VECTOR_PIECES = [[0, 1], [0, 1], [0], [0], [0], [0], [0], [0]]
 UNIT = 256
 FUSED = 512
@@ -55,8 +55,8 @@ def tile_picked_gatv_none_e_kernel(tc, xT, w1_words, w1_scales, score, offs, pos
         nc.gpsimd.memset(w_scales[:].rearrange("p z n -> p (z n)").bitcast(I32), 0)
         make_identity(nc, ident[:])
         nc.sync.dma_start(planes[0][:], x_rows[0, 0])
-        nc.scalar.dma_start(raw[0:P:8, 0 : 32 * D].rearrange("s (d c) -> s d c", c=32), score[:, 0, :].rearrange("d (s c) -> s d c", c=32))
         nc.sync.dma_start(offs_t[:], offs)
+        nc.sync.dma_start(raw[0:P:8, 0 : 32 * D].rearrange("s (d c) -> s d c", c=32), score[:, 0, :].rearrange("d (s c) -> s d c", c=32))
         for q in range(4):
             nc.scalar.dma_start(
                 w_scales[32 * q : 32 * q + 4, :, :].bitcast(I32),
@@ -71,8 +71,8 @@ def tile_picked_gatv_none_e_kernel(tc, xT, w1_words, w1_scales, score, offs, pos
 
         nc.vector.transpose(scores[:], raw[:])
         by_target = scores[:].rearrange("p (d j e) -> p j d e", j=PER, e=8)[:, :, 0:D, 0]
-        top = keep.tile([P, PER], F32, name="top")
-        shifted = keep.tile([P, PER, D], F32, name="shifted")
+        top = keep.tile([P, PER], F32, name="top", align_bytes=64)
+        shifted = keep.tile([P, PER, D], F32, name="shifted", align_bytes=64)
         expd = keep.tile([P, PER, D], F32, name="expd")
         total = keep.tile([P, PER], F32, name="total")
         inverse = keep.tile([P, PER], F32, name="inverse")
@@ -131,6 +131,8 @@ def tile_picked_gatv_none_e_kernel(tc, xT, w1_words, w1_scales, score, offs, pos
 
             for t0 in (0, 2):
                 tags = ["picked%d_%d_%d" % (z, t0, i) for i in range(len(pieces))]
+                if (z, t0) == (0, 0):
+                    tags = ["scores", "top", "shifted"]
                 for i in VECTOR_PIECES[4 * z + t0]:
                     if z == 1 and t0 == 0:
                         tags[i] = "woven0_%d" % (len(SLICES[0]) - 1 - i)

@@ -57,13 +57,13 @@ def tile_picked_gatv_none_e_kernel(tc, xT, w1_words, w1_scales, score, offs, pos
         nc.sync.dma_start(planes[0][:], x_rows[0, 0])
         nc.sync.dma_start(offs_t[:], offs)
         nc.sync.dma_start(raw[0:P:8, 0 : 32 * D].rearrange("s (d c) -> s d c", c=32), score[:, 0, :].rearrange("d (s c) -> s d c", c=32))
+        for j in range(1, 4 * PASSES):
+            nc.sync.dma_start(planes[j][:], x_rows[j // 4, j % 4])
         for q in range(4):
-            nc.scalar.dma_start(
+            nc.sync.dma_start(
                 w_scales[32 * q : 32 * q + 4, :, :].bitcast(I32),
                 w1_scales[:, 4 * q : 4 * q + 4, :].rearrange("z r n -> r z n").bitcast(I32),
             )
-        for j in range(1, 4 * PASSES):
-            nc.sync.dma_start(planes[j][:], x_rows[j // 4, j % 4])
         for z in range(PASSES):
             nc.sync.dma_start(w_words[z][:], w1_words[z])
         for tile, src in zip(pos_t, (pos1, pos2, pos3)):

@@ -92,10 +92,12 @@ def tile_picked_gatv_none_e_kernel(tc, xT, w1_words, w1_scales, score, offs, pos
 
         first_rows = keep.tile([P, FUSED], F32, name="first_rows")
         nc.vector.tensor_copy(first_rows[:], weight_rows[0][:, 0:FUSED])
+        second_rows = keep.tile([P, UNIT], F32, name="second_rows")
+        nc.vector.tensor_copy(second_rows[:], weight_rows[1][:, UNIT:V])
 
         codes, scales = [], []
         front = [bank(D + i) for i in range(4)]
-        back = [bank(D + 4), None]
+        back = [None, None]
 
         def multiply(acc, b, z, j0, n, base, start, stop):
             s = [lo <= j0 < lo + width for lo, width in SLICES[z]].index(True)
@@ -125,7 +127,6 @@ def tile_picked_gatv_none_e_kernel(tc, xT, w1_words, w1_scales, score, offs, pos
                     j0, n = SLICES[z][s]
                     if s < 2:
                         multiply(front[0], 0, 1, j0, n, 0, False, s == 1)
-                        multiply(back[0], 1, 1, j0, n, 0, False, s == 1)
                     else:
                         multiply(front[s - 1], 0, 1, j0, n, j0, False, True)
 
@@ -147,7 +148,11 @@ def tile_picked_gatv_none_e_kernel(tc, xT, w1_words, w1_scales, score, offs, pos
                     for i, (s, c0, n) in enumerate(pieces):
                         j0 = SLICES[z][s][0] + c0
                         looked_up = planes[j][:].indirect(offs_t[:, j0 // 16 : (j0 + n) // 16])
-                        if (z, t0, i) == (1, 2, 0):
+                        if (j, i) == (7, 2):
+                            m = n // 2
+                            nc.vector.tensor_copy(picked[i][:, e, 0:m], planes[j][:].indirect(offs_t[:, j0 // 16 : (j0 + m) // 16]))
+                            nc.scalar.activation(picked[i][:, e, m:n], planes[j][:].indirect(offs_t[:, (j0 + m) // 16 : (j0 + n) // 16]), ACT.Copy)
+                        elif (z, t0, i) == (1, 2, 0):
                             nc.vector.tensor_copy(woven[s][:, :, t0 + e], looked_up)
                         elif i in VECTOR_PIECES[j]:
                             nc.vector.tensor_copy(picked[i][:, e, :], looked_up)
@@ -170,7 +175,6 @@ def tile_picked_gatv_none_e_kernel(tc, xT, w1_words, w1_scales, score, offs, pos
                 for s in range(2, len(SLICES[1])):
                     j0, n = SLICES[1][s]
                     multiply(front[s - 1], 0, 0, j0, n, j0, True, False)
-                multiply(back[0], 1, 0, 0, 512, 0, True, False)
 
         y = [
             keep.tile([P, S], F32, name="y0", align_bytes=64),
@@ -178,9 +182,12 @@ def tile_picked_gatv_none_e_kernel(tc, xT, w1_words, w1_scales, score, offs, pos
         ]
         nc.scalar.copy(y[0][:, 0:512], front[0][:])
         nc.vector.tensor_copy(y[0][:, 512:768], front[1][:, 0:256])
-        nc.scalar.copy(y[0][:, 768:896], front[2][:, 0:128])
+        nc.vector.tensor_copy(y[0][:, 768:896], front[2][:, 0:128])
         nc.scalar.copy(y[0][:, 896:1024], front[3][:, 0:128])
-        nc.vector.tensor_copy(y[1][:, 0:512], back[0][:])
+        back[0] = bank(D + 1)
+        multiply(back[0], 1, 0, 0, 512, 0, True, False)
+        for j0, n in SLICES[1][:2]:
+            multiply(back[0], 1, 1, j0, n, 0, False, j0 + n == 512)
         back[1] = bank(D + 2)
         multiply(back[1], 1, 0, 512, 512, 512, True, False)
         for j0, n in SLICES[1][2:]:
@@ -193,12 +200,12 @@ def tile_picked_gatv_none_e_kernel(tc, xT, w1_words, w1_scales, score, offs, pos
             name = "%s%d_%d_%d" % (kind, b, d, v0)
             return keep.tile([P, n], F32, name=name, tag=tag or name)
 
-        def fetch(engine, b, d, v0, n, tag=None):
-            got = fresh("fetched", b, d, v0, n, tag)
+        def fetch(engine, b, d, v0, n, tag=None, into=None):
+            got = fresh("fetched", b, d, v0, n, tag) if into is None else into
             if engine == "scalar":
-                nc.scalar.activation(got[:], look_up(b, d, v0, n), ACT.Copy)
+                nc.scalar.activation(got[:, 0:n], look_up(b, d, v0, n), ACT.Copy)
             else:
-                nc.vector.tensor_copy(got[:], look_up(b, d, v0, n))
+                nc.vector.tensor_copy(got[:, 0:n], look_up(b, d, v0, n))
             return got
 
         def fused(b, v0, n, tag=None, into=None):
@@ -208,7 +215,7 @@ def tile_picked_gatv_none_e_kernel(tc, xT, w1_words, w1_scales, score, offs, pos
 
         def weigh(got, b, d, v0, n, tag=None, into=None):
             term = fresh("term", b, d, v0, n, tag) if into is None else into
-            nc.vector.tensor_tensor(term[:], got, weight_rows[d][:, v0 : v0 + n], ALU.mult)
+            nc.vector.tensor_tensor(term[:, 0:n], got, weight_rows[d][:, v0 : v0 + n], ALU.mult)
             return term
 
         def add(engine, kind, one, other, b, v0, n, tag=None):
@@ -220,40 +227,36 @@ def tile_picked_gatv_none_e_kernel(tc, xT, w1_words, w1_scales, score, offs, pos
             nc.sync.dma_start(out[b * P : (b + 1) * P, v0 : v0 + n], result[:])
 
         n = UNIT
+        h = n // 2
         g01 = fetch("scalar", 0, 1, 0, n)
         g11 = fetch("scalar", 0, 1, n, n)
+        nc.scalar.copy(y[1][:, 0:512], back[0][:])
         nc.scalar.copy(y[1][:, 512:1024], back[1][:])
-        g02 = fetch("scalar", 0, 2, 0, n)
         g20 = fetch("scalar", 1, 0, 0, n)
         g21 = fetch("scalar", 1, 1, 0, n)
         g22 = fetch("scalar", 1, 2, 0, n)
         g31 = fetch("scalar", 1, 1, n, n)
-        g32 = [fetch("scalar", 1, 2, n + c0, n // 2) for c0 in (0, n // 2)]
+        g32 = [fetch("scalar", 1, 2, n + c0, h) for c0 in (0, h)]
         t0 = fused(0, 0, FUSED)
-        partial = keep.tile([P, V], F32, name="partial0")
+        t1 = keep.tile([P, V], F32, name="second0")
+        weigh(g01[:], 0, 1, 0, n, into=t1[:, 0:n])
+        nc.gpsimd.tensor_tensor(t1[:, n:V], g11[:], second_rows[:], ALU.mult)
+        partial = add(nc.gpsimd, "partial", t0[:], t1[:], 0, 0, V)
+        g2 = [fetch("vector", 0, 2, v0, n) for v0 in (0, n)]
         t2 = keep.tile([P, V], F32, name="third0")
-        t01 = weigh(g01[:], 0, 1, 0, n)
-        nc.gpsimd.tensor_tensor(partial[:, 0:n], t0[:, 0:n], t01[:], ALU.add)
-        t11 = weigh(g11[:], 0, 1, n, n)
-        nc.gpsimd.tensor_tensor(partial[:, n:V], t0[:, n:V], t11[:], ALU.add)
-        g12 = fetch("vector", 0, 2, n, n, tag="fetched0_1_0")
-        h = n // 2
-        g30 = [fetch("vector", 1, 0, n, h, tag="fetched0_1_256")]
-        weigh(g02[:], 0, 2, 0, n, into=t2[:, 0:n])
-        weigh(g12[:], 0, 2, n, n, into=t2[:, n:V])
-        g30.append(fetch("vector", 1, 0, n + h, h, tag="fetched0_2_0"))
+        weigh(g2[0][:], 0, 2, 0, n, into=t2[:, 0:n])
+        weigh(g2[1][:], 0, 2, n, n, into=t2[:, n:V])
+        first3 = fetch("vector", 1, 0, n, n, tag="fetched0_2_0")
         store(add(nc.gpsimd, "result", partial[:], t2[:], 0, 0, V), 0, 0, V)
         t20 = weigh(g20[:], 1, 0, 0, n)
-        t30 = keep.tile([P, n], F32, name="first3")
-        weigh(g30[0][:], 1, 0, n, h, into=t30[:, 0:h])
-        weigh(g30[1][:], 1, 0, n + h, h, into=t30[:, h:n])
         t21 = weigh(g21[:], 1, 1, 0, n)
+        p2 = add(nc.gpsimd, "partial", t20[:], t21[:], 1, 0, n)
+        t30 = weigh(first3[:], 1, 0, n, n)
         t22 = weigh(g22[:], 1, 2, 0, n)
-        p2 = add(nc.vector, "partial", t20[:], t21[:], 1, 0, n)
         t31 = weigh(g31[:], 1, 1, n, n)
-        store(add(nc.vector, "result", p2[:], t22[:], 1, 0, n), 1, 0, n)
         last = [weigh(g32[0][:], 1, 2, n, h)]
         p3 = add(nc.vector, "partial", t30[:], t31[:], 1, n, n)
         last.append(weigh(g32[1][:], 1, 2, n + h, h))
+        store(add(nc.vector, "result", p2[:], t22[:], 1, 0, n), 1, 0, n)
         for i, c0 in enumerate((0, h)):
             store(add(nc.vector, "result", p3[:, c0 : c0 + h], last[i][:], 1, n + c0, h), 1, n + c0, h)

@@ -249,14 +249,14 @@ def tile_picked_gatv_none_e_kernel(tc, xT, w1_words, w1_scales, score, offs, pos
         first3 = fetch("vector", 1, 0, n, n, tag="fetched0_2_0")
         store(add(nc.gpsimd, "result", partial[:], t2[:], 0, 0, V), 0, 0, V)
         t20 = weigh(g20[:], 1, 0, 0, n)
-        t21 = weigh(g21[:], 1, 1, 0, n)
-        p2 = add(nc.gpsimd, "partial", t20[:], t21[:], 1, 0, n)
         t30 = weigh(first3[:], 1, 0, n, n)
+        t21 = weigh(g21[:], 1, 1, 0, n)
         t22 = weigh(g22[:], 1, 2, 0, n)
+        p2 = add(nc.vector, "partial", t20[:], t21[:], 1, 0, n)
         t31 = weigh(g31[:], 1, 1, n, n)
+        store(add(nc.vector, "result", p2[:], t22[:], 1, 0, n), 1, 0, n)
         last = [weigh(g32[0][:], 1, 2, n, h)]
         p3 = add(nc.vector, "partial", t30[:], t31[:], 1, n, n)
         last.append(weigh(g32[1][:], 1, 2, n + h, h))
-        store(add(nc.vector, "result", p2[:], t22[:], 1, 0, n), 1, 0, n)
         for i, c0 in enumerate((0, h)):
             store(add(nc.vector, "result", p3[:, c0 : c0 + h], last[i][:], 1, n + c0, h), 1, n + c0, h)

@@ -65,7 +65,7 @@ def tile_picked_gatv_none_e_kernel(tc, xT, w1_words, w1_scales, score, offs, pos
                 w1_scales[:, 4 * q : 4 * q + 4, :].rearrange("z r n -> r z n").bitcast(I32),
             )
         for z in range(PASSES):
-            nc.sync.dma_start(w_words[z][:], w1_words[z])
+            nc.sync.dma_start(w_words[z][:].bitcast(I32), w1_words[z].bitcast(I32))
         for tile, src in zip(pos_t, (pos1, pos2, pos3)):
             nc.sync.dma_start(tile[:], src)
 

from contextlib import ExitStack

import concourse.mybir as mybir
from concourse.masks import make_identity

K, T, S, D, V, N = 1024, 2048, 1024, 3, 512, 256
FLOPS = 2 * K * N * S
BYTES = K * T * 4 + N * V * 4 + K * N // 2 + K * N // 32 + D * V * 4

F32 = mybir.dt.float32
BF16 = mybir.dt.bfloat16
I32 = mybir.dt.int32
U32 = mybir.dt.uint32
U16 = mybir.dt.uint16
U8 = mybir.dt.uint8
FP8X4 = mybir.dt.float8_e4m3fn_x4
FP4X4 = mybir.dt.float4_e2m1fn_x4
ALU = mybir.AluOpType
ACT = mybir.ActivationFunctionType
AXIS = mybir.AxisListType

P = 128
PASSES = K // 512
BLOCKS = N // P
BANK = 512
PER = V // P
SLICES = [[(0, 512), (512, 512)], [(0, 256), (256, 256), (512, 256), (768, 128), (896, 128)]]
PIECES = [[(0, 0, 256), (0, 256, 256), (1, 0, 512)], [(0, 0, 256), (1, 0, 256), (2, 0, 256), (3, 0, 128), (4, 0, 128)]]
VECTOR_PIECES = [[0, 1], [0, 1], [0], [0], [0], [0], [0], [0]]
UNIT = 256
FUSED = 512


def tile_picked_gatv_none_e_kernel(tc, xT, w1_words, w1_scales, score, offs, pos1, pos2, pos3, out):
    nc = tc.nc
    with ExitStack() as ctx:
        lists = ctx.enter_context(tc.tile_pool(name="lists", bufs=1))
        keep = ctx.enter_context(tc.tile_pool(name="keep", bufs=1))
        psum = ctx.enter_context(tc.psum_pool(name="psum", bufs=1))

        def bank(i):
            return psum.tile([P, BANK], F32, name="bank%d" % i, tag="bank%d" % i)

        x_rows = xT.rearrange("(z p t) c -> z t p c", p=P, t=4)
        offs_t = lists.tile([P, S // 16], U16, name="offs_t")
        pos_t = [lists.tile([P, V // 16], U16, name="pos_t%d" % d) for d in range(D)]
        raw = keep.tile([P, P], F32, name="raw", align_bytes=64)
        scores = keep.tile([P, P], F32, name="scores", align_bytes=64)
        w_words = [keep.tile([P, 2 * N], U8, name="w_words%d" % z, align_bytes=64) for z in range(PASSES)]
        w_scales = keep.tile([P, PASSES, N], U8, name="w_scales", align_bytes=64)
        ident = keep.tile([P, P], F32, name="ident")
        planes = [keep.tile([P, T], F32, name="plane%d" % j) for j in range(4 * PASSES)]

        nc.gpsimd.memset(raw[:], 0.0)
        nc.gpsimd.memset(w_scales[:].rearrange("p z n -> p (z n)").bitcast(I32), 0)
        make_identity(nc, ident[:])
        nc.sync.dma_start(planes[0][:], x_rows[0, 0])
        nc.sync.dma_start(offs_t[:], offs)
        nc.sync.dma_start(raw[0:P:8, 0 : 32 * D].rearrange("s (d c) -> s d c", c=32), score[:, 0, :].rearrange("d (s c) -> s d c", c=32))
        for j in range(1, 4 * PASSES):
            nc.sync.dma_start(planes[j][:], x_rows[j // 4, j % 4])
        for q in range(4):
            nc.sync.dma_start(
                w_scales[32 * q : 32 * q + 4, :, :].bitcast(I32),
                w1_scales[:, 4 * q : 4 * q + 4, :].rearrange("z r n -> r z n").bitcast(I32),
            )
        for z in range(PASSES):
            nc.sync.dma_start(w_words[z][:].bitcast(I32), w1_words[z].bitcast(I32))
        for tile, src in zip(pos_t, (pos1, pos2, pos3)):
            nc.sync.dma_start(tile[:], src)

        nc.vector.transpose(scores[:], raw[:])
        by_target = scores[:].rearrange("p (d j e) -> p j d e", j=PER, e=8)[:, :, 0:D, 0]
        top = keep.tile([P, PER], F32, name="top", align_bytes=64)
        shifted = keep.tile([P, PER, D], F32, name="shifted", align_bytes=64)
        expd = keep.tile([P, PER, D], F32, name="expd")
        total = keep.tile([P, PER], F32, name="total")
        inverse = keep.tile([P, PER], F32, name="inverse")
        weight = keep.tile([P, PER, D], F32, name="weight")
        nc.vector.tensor_reduce(top[:], by_target, AXIS.X, ALU.max)
        nc.vector.tensor_tensor(shifted[:], by_target, top[:].unsqueeze(2).to_broadcast([P, PER, D]), ALU.subtract)
        nc.scalar.activation(expd[:], shifted[:], ACT.Exp)
        nc.vector.tensor_reduce(total[:], expd[:], AXIS.X, ALU.add)
        nc.vector.reciprocal(inverse[:], total[:])
        nc.vector.tensor_tensor(weight[:], expd[:], inverse[:].unsqueeze(2).to_broadcast([P, PER, D]), ALU.mult)
        weight_rows = []
        for d in range(D):
            spread = bank(d)
            for j in range(PER):
                nc.tensor.transpose(spread[:].rearrange("p (q s c) -> p s q c", q=4, c=32)[:, j], weight[:, j, d : d + 1].to_broadcast([P, P]), ident[:])
            weight_rows.append(spread)

        first_rows = keep.tile([P, FUSED], F32, name="first_rows")
        nc.vector.tensor_copy(first_rows[:], weight_rows[0][:, 0:FUSED])
        second_rows = keep.tile([P, UNIT], F32, name="second_rows")
        nc.vector.tensor_copy(second_rows[:], weight_rows[1][:, UNIT:V])

        codes, scales = [], []
        front = [bank(D + i) for i in range(4)]
        back = [None, None]

        def multiply(acc, b, z, j0, n, base, start, stop):
            s = [lo <= j0 < lo + width for lo, width in SLICES[z]].index(True)
            c0 = j0 - SLICES[z][s][0]
            nc.tensor.matmul_mx(
                out=acc[:, j0 - base : j0 - base + n],
                lhsT=w_words[z][:, 2 * P * b : 2 * P * (b + 1)].bitcast(FP4X4),
                lhsT_scale=w_scales[:, z, P * b : P * (b + 1)],
                rhs=codes[z][s][:, c0 : c0 + n].bitcast(FP8X4),
                rhs_scale=scales[z][s][:, c0 : c0 + n],
                start=start,
                stop=stop,
            )

        for z in range(PASSES):
            count = len(SLICES[z])
            pieces = PIECES[z]
            woven = [keep.tile([P, n, 4], BF16, name="woven%d_%d" % (z, s), align_bytes=64) for s, (j0, n) in enumerate(SLICES[z])]
            codes.append([keep.tile([P, n], U32, name="codes%d_%d" % (z, s), align_bytes=64) for s, (j0, n) in enumerate(SLICES[z])])
            scales.append([keep.tile([P, n], U8, name="scales%d_%d" % (z, s), align_bytes=64) for s, (j0, n) in enumerate(SLICES[z])])

            def finish(s):
                nc.vector.quantize_mx(
                    out=codes[z][s][:].bitcast(FP8X4), scales=scales[z][s][:], in_=woven[s][:].rearrange("p n t -> p (n t)")
                )
                if z == 1:
                    j0, n = SLICES[z][s]
                    if s < 2:
                        multiply(front[0], 0, 1, j0, n, 0, False, s == 1)
                    else:
                        multiply(front[s - 1], 0, 1, j0, n, j0, False, True)

            for t0 in (0, 2):
                tags = ["picked%d_%d_%d" % (z, t0, i) for i in range(len(pieces))]
                if (z, t0) == (0, 0):
                    tags = ["scores", "top", "shifted"]
                for i in VECTOR_PIECES[4 * z + t0]:
                    if z == 1 and t0 == 0:
                        tags[i] = "woven0_%d" % (len(SLICES[0]) - 1 - i)
                    if t0 == 2:
                        tags[i] = "picked%d_0_%d" % (z, len(pieces) - 1 - i)
                picked = [
                    None if (z, t0, i) == (1, 2, 0) else keep.tile([P, 2, n], BF16, name="picked%d_%d_%d" % (z, t0, i), tag=tags[i], align_bytes=64)
                    for i, (s, c0, n) in enumerate(pieces)
                ]
                for e in range(2):
                    j = 4 * z + t0 + e
                    for i, (s, c0, n) in enumerate(pieces):
                        j0 = SLICES[z][s][0] + c0
                        looked_up = planes[j][:].indirect(offs_t[:, j0 // 16 : (j0 + n) // 16])
                        if (j, i) == (7, 2):
                            m = n // 2
                            nc.vector.tensor_copy(picked[i][:, e, 0:m], planes[j][:].indirect(offs_t[:, j0 // 16 : (j0 + m) // 16]))
                            nc.scalar.activation(picked[i][:, e, m:n], planes[j][:].indirect(offs_t[:, (j0 + m) // 16 : (j0 + n) // 16]), ACT.Copy)
                        elif (z, t0, i) == (1, 2, 0):
                            nc.vector.tensor_copy(woven[s][:, :, t0 + e], looked_up)
                        elif i in VECTOR_PIECES[j]:
                            nc.vector.tensor_copy(picked[i][:, e, :], looked_up)
                        else:
                            nc.scalar.activation(picked[i][:, e, :], looked_up, ACT.Copy)
                done = 0
                for i, (s, c0, n) in enumerate(pieces):
                    if (z, t0, i) == (1, 2, 0):
                        continue
                    if (z, t0) == (1, 2) and i >= len(pieces) - 2:
                        nc.scalar.copy(woven[s][:, c0 : c0 + n, t0 : t0 + 2], picked[i][:].rearrange("p e n -> p n e"))
                    else:
                        nc.vector.tensor_copy(woven[s][:, c0 : c0 + n, t0 : t0 + 2], picked[i][:].rearrange("p e n -> p n e"))
                    if t0 == 2 and s > done:
                        finish(done)
                        done = done + 1
            finish(count - 1)
            if z == 0:
                multiply(front[0], 0, 0, 0, 512, 0, True, False)
                for s in range(2, len(SLICES[1])):
                    j0, n = SLICES[1][s]
                    multiply(front[s - 1], 0, 0, j0, n, j0, True, False)

        y = [
            keep.tile([P, S], F32, name="y0", align_bytes=64),
            keep.tile([P, S], F32, name="y1", tag="woven1_%d" % (len(SLICES[1]) - 1), align_bytes=64),
        ]
        nc.scalar.copy(y[0][:, 0:512], front[0][:])
        nc.vector.tensor_copy(y[0][:, 512:768], front[1][:, 0:256])
        nc.vector.tensor_copy(y[0][:, 768:896], front[2][:, 0:128])
        nc.scalar.copy(y[0][:, 896:1024], front[3][:, 0:128])
        back[0] = bank(D + 1)
        multiply(back[0], 1, 0, 0, 512, 0, True, False)
        for j0, n in SLICES[1][:2]:
            multiply(back[0], 1, 1, j0, n, 0, False, j0 + n == 512)
        back[1] = bank(D + 2)
        multiply(back[1], 1, 0, 512, 512, 512, True, False)
        for j0, n in SLICES[1][2:]:
            multiply(back[1], 1, 1, j0, n, 512, False, j0 + n == S)

        def look_up(b, d, v0, n):
            return y[b][:].indirect(pos_t[d][:, v0 // 16 : (v0 + n) // 16])

        def fresh(kind, b, d, v0, n, tag=None):
            name = "%s%d_%d_%d" % (kind, b, d, v0)
            return keep.tile([P, n], F32, name=name, tag=tag or name)

        def fetch(engine, b, d, v0, n, tag=None, into=None):
            got = fresh("fetched", b, d, v0, n, tag) if into is None else into
            if engine == "scalar":
                nc.scalar.activation(got[:, 0:n], look_up(b, d, v0, n), ACT.Copy)
            else:
                nc.vector.tensor_copy(got[:, 0:n], look_up(b, d, v0, n))
            return got

        def fused(b, v0, n, tag=None, into=None):
            term = fresh("term", b, 0, v0, n, tag) if into is None else into
            nc.vector.tensor_tensor(term[:], look_up(b, 0, v0, n), first_rows[:, v0 : v0 + n], ALU.mult)
            return term

        def weigh(got, b, d, v0, n, tag=None, into=None):
            term = fresh("term", b, d, v0, n, tag) if into is None else into
            nc.vector.tensor_tensor(term[:, 0:n], got, weight_rows[d][:, v0 : v0 + n], ALU.mult)
            return term

        def add(engine, kind, one, other, b, v0, n, tag=None):
            total = fresh(kind, b, 0, v0, n, tag)
            engine.tensor_tensor(total[:], one, other, ALU.add)
            return total

        def store(result, b, v0, n):
            nc.sync.dma_start(out[b * P : (b + 1) * P, v0 : v0 + n], result[:])

        n = UNIT
        h = n // 2
        g01 = fetch("scalar", 0, 1, 0, n)
        g11 = fetch("scalar", 0, 1, n, n)
        nc.scalar.copy(y[1][:, 0:512], back[0][:])
        nc.scalar.copy(y[1][:, 512:1024], back[1][:])
        g20 = fetch("scalar", 1, 0, 0, n)
        g21 = fetch("scalar", 1, 1, 0, n)
        g22 = fetch("scalar", 1, 2, 0, n)
        g31 = fetch("scalar", 1, 1, n, n)
        g32 = [fetch("scalar", 1, 2, n + c0, h) for c0 in (0, h)]
        t0 = fused(0, 0, FUSED)
        t1 = keep.tile([P, V], F32, name="second0")
        weigh(g01[:], 0, 1, 0, n, into=t1[:, 0:n])
        nc.gpsimd.tensor_tensor(t1[:, n:V], g11[:], second_rows[:], ALU.mult)
        partial = add(nc.gpsimd, "partial", t0[:], t1[:], 0, 0, V)
        g2 = [fetch("vector", 0, 2, v0, n) for v0 in (0, n)]
        t2 = keep.tile([P, V], F32, name="third0")
        weigh(g2[0][:], 0, 2, 0, n, into=t2[:, 0:n])
        weigh(g2[1][:], 0, 2, n, n, into=t2[:, n:V])
        first3 = fetch("vector", 1, 0, n, n, tag="fetched0_2_0")
        store(add(nc.gpsimd, "result", partial[:], t2[:], 0, 0, V), 0, 0, V)
        t20 = weigh(g20[:], 1, 0, 0, n)
        t30 = weigh(first3[:], 1, 0, n, n)
        t21 = weigh(g21[:], 1, 1, 0, n)
        t22 = weigh(g22[:], 1, 2, 0, n)
        p2 = add(nc.vector, "partial", t20[:], t21[:], 1, 0, n)
        t31 = weigh(g31[:], 1, 1, n, n)
        store(add(nc.vector, "result", p2[:], t22[:], 1, 0, n), 1, 0, n)
        last = [weigh(g32[0][:], 1, 2, n, h)]
        p3 = add(nc.vector, "partial", t30[:], t31[:], 1, n, n)
        last.append(weigh(g32[1][:], 1, 2, n + h, h))
        for i, c0 in enumerate((0, h)):
            store(add(nc.vector, "result", p3[:, c0 : c0 + h], last[i][:], 1, n + c0, h), 1, n + c0, h)
